import numpy as np, ml_dtypes
CORES = [16,18,20,22]
N = 4
BF = ml_dtypes.bfloat16
def gentries(a):
    return np.ascontiguousarray(a.reshape(8, 16, -1).transpose(0, 2, 1)).reshape(8, -1)
def gtable(e):
    e = np.asarray(e); return np.ascontiguousarray(e.reshape(8, -1, 16).transpose(0, 2, 1)).reshape(128, -1).astype(np.int32)
T, C, R, S, VI = 4096, 2048, 64, 16, 6
def parts(rng):
    book = rng.integers(0, T, (N, 8, 16, C)); mix = rng.choice(np.array([0.2, 0.5, 0.8, 1.0]), (N, 8, 1, 1))
    W = np.minimum((256 * ((1 - mix) * rng.random((N, 8, 1, T)) + mix * rng.random((N, 8, 16, T)))).astype(np.int64), 255)
    wt = rng.integers(0, 256, (N, 8, 16)); sg = rng.integers(0, T, (N, 8, T)); sg[:, ::2] = np.argsort(rng.random((N, 4, T)), axis=-1)
    return book, W, wt, sg, rng.integers(0, C, (N, 8, S, R))
def pack(book, W, wt, sg, km):
    return {"book": np.ascontiguousarray(book.reshape(N, 128, C)).astype(np.int32), "tru": np.ascontiguousarray(W.reshape(N, 128, T)).astype(np.float32).astype(BF),
            "wt": np.ascontiguousarray(wt.reshape(N, 128, 1)).astype(np.int32), "sg0": np.stack([gtable(v) for v in sg]), "km0": np.stack([gtable(v.reshape(8, -1)) for v in km])}
def setup_inputs(rng):
    book, W, wt, sg, km = parts(rng)
    km[:, :, :, 3] = km[:, :, :1, 3]; km[:, :, :, 7] = km[:, :, :, 5]; km[:, :, :, 9] = km[:, :, :, 5]
    return pack(book, W, wt, sg, km)
def setup_inputs_spread(rng):
    book, W, wt, sg, km = parts(rng)
    W = np.minimum((np.exp2(8 * rng.random((N, 8, 1, T))) * rng.random((N, 8, 16, T)) * (rng.random((N, 8, 1, T)) > 0.0625)).astype(np.int64), 255)
    W[:, 1::2] = 255 - W[:, 1::2]; wt = np.minimum(np.exp2(8 * rng.random((N, 8, 16))).astype(np.int64), 255)
    book[:, :, ::2] = np.minimum((T * rng.random((N, 8, 8, C)) ** 3).astype(np.int64), T - 1)
    sg[:, ::3] = np.minimum((T * rng.random((N, 3, T)) ** 2).astype(np.int64), T - 1)
    km = np.minimum((C * rng.random((N, 8, S, R)) ** 2).astype(np.int64), C - 1)
    return pack(book, W, wt, sg, km)
def setup_inputs_ends(rng):
    book, W, wt, sg, km = parts(rng)
    kind = rng.random((N, 8, 1, T)); one = (np.arange(16)[:, None] == rng.integers(0, 16, (N, 8, 1, T))).astype(np.int64)
    bits = 255 * rng.integers(0, 2, (N, 8, 16, T))
    W = np.where(kind < 0.2, 255, np.where(kind < 0.32, 255 - one, np.where(kind < 0.44, 0, np.where(kind < 0.5, one, np.where(kind < 0.75, bits, W)))))
    sg = np.where(rng.random((N, 8, T)) < 0.65, (T - 1) * rng.integers(0, 2, (N, 8, T)), sg); sg[..., 0] = 0; sg[..., T - 1] = T - 1
    kc = rng.random((N, 8, 1, C)); two = (T - 1) * rng.integers(0, 2, (N, 8, 16, C))
    book = np.where(kc < 0.22, T - 1, np.where(kc < 0.33, 0, np.where(kc < 0.58, two, np.where((kc < 0.72) & (rng.random(book.shape) < 0.5), two, book))))
    book[..., 0] = (T - 1) * ((np.arange(16) + rng.integers(0, 2, (N, 8, 1))) % 2); book[..., C - 1] = T - 1
    km = np.where(rng.random(km.shape) < 0.65, (C - 1) * rng.integers(0, 2, km.shape), km)
    wt = 255 * rng.integers(0, 2, (N, 8, 16)); wt[:, :, :5] = rng.integers(0, 256, (N, 8, 5)); wt[:, 0] = 255; wt[:, 7] = 255; wt[:, 4] = 0
    for q in range(N):
        for g in range(8):
            kd = (g + q) % 4
            if q == N - 2 or (q == 0 and kd == 2) or (q == N - 1 and g == 7): kd = 0
            P = np.where(rng.permutation(16) < int(rng.integers(8, 10)), 255, 0)
            W[q, g, :, 0] = (0, 255, 255, 255 - P)[kd]; W[q, g, :, T - 1] = (255, 0, 255, P)[kd]
    km[0, :, 0, :] = 0
    km[N - 2, :, 0, :] = C - 1; km[N - 2, :, S - 1, :] = 0; km[N - 2, :, 1:S - 1, R - 1] = C - 1
    km[N - 1, 7, :, R - 1] = C - 1
    W[N - 1, 7, :, 7] = 255 * (np.arange(16) % 2); sg[N - 1, 7, 1] = 0; sg[N - 1, 7, 2] = 7; sg[N - 1, 7, T - 2] = T - 1
    e = np.full(16, 2); e[2] = T - 2; e[15] = T - 1; e[5] = 1; e[14] = 0; book[N - 1, 7, :, 600] = e
    return pack(book, W, wt, sg, km)
def setup_inputs_corners(rng):
    book, W, wt, sg, km = parts(rng); h = C // 2
    km[:, 0] = rng.integers(0, C, (N, 1, R))
    W[:, 1:3, :, :T // 2] = rng.integers(0, 100, (N, 2, 16, T // 2)); W[:, 1:3, :, T // 2:] = rng.integers(156, 256, (N, 2, 16, T - T // 2)); sg[:, 1:3] = np.arange(T)
    book[:, 1:3, :, :h] = rng.integers(T // 2, T, (N, 2, 16, h)); book[:, 1:3, :, h:] = rng.integers(0, T // 2, (N, 2, 16, C - h))
    km[:, 1] = rng.integers(0, h, (N, 1, R)); km[:, 1, S - 1] = rng.integers(h, C, (N, R))
    km[:, 2, 0] = rng.integers(0, h, (N, R)); km[:, 2, 1:] = rng.integers(h, C, (N, S - 1, R))
    book[:, 3, :, ::2] = rng.integers(0, T, (N, 1, h))
    sg[:, 4] = np.where(np.arange(T) % 2 == 0, 0, T - 1); book[:, 4] = (book[:, 4] // 2) * 2 + np.arange(C) % 2
    for q in range(N):
        m = 9 if q % 2 == 0 else 8
        W[q, 4, :, 0] = np.where(np.arange(16) < m, 10, 200); W[q, 4, :, T - 1] = np.where(np.arange(16) < m, 20, 100)
    wt[:, 5] = 0; wt[:, 7] = 255; wt[:, 6] = 255 * rng.integers(0, 2, (N, 16)); wt[:, 6, :4] = rng.integers(1, 256, (N, 4))
    few = np.concatenate([np.array([0, T - 1, 1, T - 2]), rng.permutation(T - 8)[:20] + 4]); book[:, 6] = few[book[:, 6] % 24]
    book[:, 7, 0] = T - 1; sg[:, 7, T - 1] = T - 1; W[:, 7, :, T - 1] = 255
    return pack(book, W, wt, sg, km)
def aim(rng, w, taken, m):
    V = rng.integers(0, 255, (16, 2048)); u = np.add.reduce(w[:, None] * V, axis=0) & 4095; n = ((u * u >> 5) + 37 * u) & (C - 1)
    v, i = np.unique(n, return_index=True); i = rng.permutation(i[~np.isin(v, taken)])[:m]
    return V[:, i], n[i]
def plant(rng, bk, Wg, s, cols, a, b, zero, top, rest, g):
    for j in range(R):
        kind = (j + g) % 3; one = (np.arange(16) == int(rng.integers(0, 16))).astype(np.int64); p, o = rng.permutation(16)[:2]
        pool = (rest, zero, top)[kind]; col = pool[rng.integers(0, len(pool), 16)]
        if kind == 1: p, o = int(rng.integers(1, 16)), 0
        if kind == 2: p, o = 0, int(rng.integers(1, 16))
        col[p] = a[j]; col[o] = b[j]; bk[:, cols[j]] = col
        Wg[:, s[a[j]]] = one if kind == 1 else 255
        Wg[:, s[b[j]]] = 255 - one if kind == 2 else 0
def setup_inputs_full(rng):
    book, W, wt, sg, km = parts(rng); W = np.clip(W, 1, 254); sg = np.argsort(rng.random((N, 8, T)), axis=-1); wt[:, :, 0] = 255
    for r in range(0, N - 1, 2):
        q = r + 1
        for g in range(8):
            x = rng.permutation(T); a0, b0, a1, b1 = np.array(x[:4 * R]).reshape(4, R)
            z, zero, top, rest = x[4 * R:5 * R + 1], x[5 * R + 1:5 * R + 17], x[5 * R + 17:5 * R + 33], x[5 * R + 33:]
            if g == 3: a1[7] = b0[7]; b1[9] = a0[9]
            if g == 5: a1[5] = a0[0]
            y = rng.permutation(C); O, P, X1, X = int(y[0]), int(y[1]), int(y[2]), y[3:3 + R]
            V0, n0 = aim(rng, wt[r, g], y[:3 + R], R); V1, n1 = aim(rng, wt[q, g], np.concatenate([y[:3], n0]), R + 1)
            for c in (r, q):
                W[c, g][:, sg[c, g][zero]] = 0; W[c, g][:, sg[c, g][top]] = 255
            W[r, g][:, sg[r, g][z[:R]]] = V0; book[r, g][:, X] = z[:R]; book[r, g][:, O] = zero[0]
            plant(rng, book[r, g], W[r, g], sg[r, g], n0, a0, b0, zero, top, rest, g)
            km[r, g, 0] = O; km[r, g, 1] = X
            W[q, g][:, sg[q, g][z]] = V1; book[q, g][:, n0] = z[:R]; book[q, g][:, X1] = z[R]
            book[q, g][:, O] = top[0]; book[q, g][:, P] = zero[0]; book[q, g][:, n1[R]] = top[1]
            plant(rng, book[q, g], W[q, g], sg[q, g], n1, a1, b1, zero, top, rest, g + 1)
            if g == 5: book[q, g][:, n1[0]] = a1[0]
            km[q, g, 0] = P; km[q, g, 1] = X1
    return pack(book, W, wt, sg, km)
def setup_inputs_hush(rng):
    book, W, wt, sg, km = parts(rng); q0 = int(rng.integers(0, N))
    for q in (q0, (q0 + 2) % N):
        for g in range(8):
            x = rng.permutation(T)[:3]; m = rng.permutation(T)[:3]; y = rng.permutation(C)[:3]
            hi = rng.integers(160, 255, 16) if g < 7 else np.where(rng.permutation(16) < 9, 254, 255)
            sg[q, g, x] = m; W[q, g, :, m[0]] = 0; W[q, g, :, m[1]] = 255; W[q, g, :, m[2]] = hi
            book[q, g] = np.where(book[q, g] == x[0], x[1], book[q, g]); book[q, g][:, y] = x
            wt[q, g] = rng.integers(224, 256, 16) if g < 7 else 255
            km[q, g, :, ::2] = y[1]; km[q, g, S - 1, ::2] = y[2]; km[(q - 1) % N, g, 0] = y[0]
    return pack(book, W, wt, sg, km)
def check_inputs(d):
    bad = []
    for k, lo, hi in (("book", 0, T - 1), ("tru", 0, 255), ("wt", 0, 255), ("sg0", 0, T - 1), ("km0", 0, C - 1)):
        v = np.asarray(d[k]).astype(np.float64)
        if not (np.min(v) >= lo and np.max(v) <= hi): bad.append("range of " + k)
        elif np.any(np.floor(v) != v): bad.append("whole numbers in " + k)
    return bad
def reference(book, tru, wt, sg0, km0):
    B = np.ascontiguousarray(book.astype(np.int64).reshape(N, 8, 16, C).transpose(0, 1, 3, 2))
    W = np.ascontiguousarray(tru.astype(np.float32).astype(np.int64).reshape(N, 8, 16, T).transpose(0, 1, 3, 2))
    w = wt.astype(np.int64).reshape(N, 8, 16)
    s = np.stack([gentries(v) for v in sg0]).astype(np.int64)
    K = np.stack([gentries(v) for v in km0]).astype(np.int64).reshape(N, 8, S, R)
    a = np.full((N, 8, S, R), -1, np.int64); b = np.full((N, 8, S, R), -1, np.int64)
    last = np.zeros(N, np.int64); ar = np.arange(R)
    for t in range(VI):
        new = np.zeros(N, np.int64)
        for r in range(N):
            q = (r + t) % N
            for g in range(8):
                Z = W[q, g][s[q, g]]
                y = np.min(Z[B[q, g][K[r, g].reshape(-1)]], axis=1).reshape(S, R, 16)
                con = np.add.reduce((y[1:] < y[:1]).astype(np.int64), axis=2) >= 9
                hit = np.any(con, axis=0); ks = np.where(hit, 1 + np.argmax(con, axis=0), 1 + t)
                u = np.add.reduce(y[ks, ar] * w[q, g], axis=1) & 4095
                n = ((u * u >> 5) + 37 * u + last[q]) & (C - 1)
                e = B[q, g][n]; sc = np.add.reduce(Z[e], axis=2)
                na = e[ar, np.argmax(sc, axis=1)]; nb = e[ar, np.argmin(sc, axis=1)]
                oa = np.where(hit, a[r, g, ks, ar], -1); ob = np.where(hit, b[r, g, ks, ar], -1)
                nm = np.stack([na, nb, oa, ob]); nm = np.where(nm < 0, T, nm)
                own = np.full(T + 1, R, np.int64); np.minimum.at(own, nm, np.broadcast_to(ar, (4, R))); own[T] = R
                ok = (na != nb) & (na != oa) & (na != ob) & (nb != oa) & (nb != ob) & ~np.any(own[nm] < ar, axis=0)
                old = np.array(s[q, g]); i = np.nonzero(ok)[0]; h = np.nonzero(ok & (oa >= 0))[0]
                s[q, g, na[i]] = old[nb[i]]; s[q, g, nb[i]] = old[na[i]]
                s[q, g, oa[h]] = old[ob[h]]; s[q, g, ob[h]] = old[oa[h]]
                K[r, g, ks, ar] = n; a[r, g, ks, ar] = np.where(ok, na, -1); b[r, g, ks, ar] = np.where(ok, nb, -1)
                new[q] += np.add.reduce(hit.astype(np.int64))
        last = new
    return {"yk": np.stack([gtable(v.reshape(8, -1)) for v in K]).astype(np.float32), "ya": np.stack([gtable(v.reshape(8, -1)) for v in a]).astype(np.float32),
            "yb": np.stack([gtable(v.reshape(8, -1)) for v in b]).astype(np.float32), "ys": s.astype(np.float32)}

@@ -1,0 +1,515 @@
+from concourse.mybir import AluOpType as A, AxisListType as X, ActivationFunctionType as F
+
+VI = 6
+CB = 17500
+RW = [256, 192, 128, 64]
+NB = [0, 1024, 1792, 2304]
+
+SB = {
+    "bk": (2560, "int32"), "trus": (4096, "bfloat16"), "sgi": (256, "int32"), "sl": (256, "uint16"), "kmi": (64, "int32"),
+    "kmf": (64, "float32"), "wti": (8, "int32"), "wtf": (8, "float32"),
+    "z": (4352, "bfloat16"), "stab": (4352, "float32"), "iot": (4096, "float32"),
+    "gg": (16384, "bfloat16"), "scn": (17408, "bfloat16"), "rst": (4096, "bfloat16"),
+    "tt": (1024, "uint16"), "lt": (1024, "bfloat16"), "val": (68, "float32"), "m": (8, "float32"), "m2": (8, "float32"),
+    "nh": (8, "float32"), "off": (4, "uint16"), "ysel": (64, "bfloat16"), "um": (64, "float32"), "us": (64, "float32"),
+    "ui": (8, "int32"), "ua": (8, "int32"), "ux": (8, "float32"), "uy": (8, "float32"), "uz": (8, "int32"), "un": (8, "int32"),
+    "nl": (8, "uint16"), "nf": (8, "float32"), "e2": (64, "uint16"), "zg": (1024, "bfloat16"), "tr": (1024, "float32"),
+    "ohk": (128, "float32"), "kf": (64, "float32"), "kd": (64, "float32"), "kd2": (64, "float32"), "kd3": (64, "float32"),
+    "pr": (128, "float32"), "prj": (128, "float32"), "old0": (16, "float32"), "old": (16, "float32"), "owo": (8, "float32"),
+    "has": (8, "float32"), "rr": (128, "float32"),
+    "oth": (256, "float32"), "kab": (128, "float32"), "kss": (128, "float32"), "ki": (8, "int32"), "ka": (8, "int32"),
+    "ofn": (8, "uint16"), "om": (128, "float32"), "osn": (128, "float32"), "ne": (2560, "bfloat16"), "ns": (2560, "bfloat16"),
+    "acc": (8, "float32"), "pd": (16, "float32"), "pdo": (8, "float32"), "dv": (16, "float32"), "da": (16, "float32"),
+    "zg2": (256, "bfloat16"), "sg2": (256, "float32"), "own1": (16, "float32"), "nw": (16, "float32"),
+    "ad": (128, "float32"), "ad2": (128, "float32"), "hit": (8, "bfloat16"), "cc": (8, "float32"),
+    "snk": (64, "float32"), "sna": (128, "float32"), "lnk": (64, "float32"), "lna": (128, "float32"),
+    "kint": (64, "int32"), "kin2": (64, "int32"), "fa": (128, "float32"),
+    "pi": (8, "int32"), "pq": (8, "int32"), "pc": (16, "float32"), "selc": (2048, "bfloat16"),
+    "sels": (2048, "bfloat16"), "gi": (128, "float32"), "g8": (8, "float32"), "gbf": (128, "float32"), "wb": (128, "bfloat16"),
+    "idt": (128, "float32"), "idb": (128, "bfloat16"), "vs": (128, "float32"), "rev": (128, "float32"), "r16": (128, "float32"),
+    "mk": (128, "float32"), "w68t": (68, "float32"), "w68": (68, "float32"), "w128": (128, "float32"), "j16t": (64, "float32"),
+    "j16": (64, "float32"), "rk2": (128, "float32"), "rk": (128, "float32"), "ra": (128, "float32"), "rep4": (8, "uint16"),
+    "rep16": (8, "uint16"), "repw": (8, "uint16"), "it8": (8, "float32"), "rw4": (8, "float32"), "msk": (2560, "bfloat16"),
+    "dut": (16, "float32"), "dum": (16, "float32"), "dm1": (8, "float32"), "cb": (128, "bfloat16"), "on": (128, "bfloat16"),
+}
+MSG = ["ab0"]
+for _t in range(VI + 1):
+    SB["k16_%d" % _t] = (64, "uint16")
+    SB["src%d" % _t] = (16, "uint16")
+    SB["dst%d" % _t] = (16, "uint16")
+    SB["ab%d" % _t] = (128, "float32")
+    SB["ks%d" % _t] = (64, "uint16")
+    SB["abs%d" % _t] = (128, "float32")
+    MSG += ["k16_%d" % _t, "ab%d" % _t, "ks%d" % _t, "abs%d" % _t]
+APART = ["bk", "trus", "sgi", "kmi", "wti", "z", "stab", "iot", "gg", "scn", "rst", "lnk", "lna", "snk", "sna"] + MSG
+POOL = {"float32": "pf32", "int32": "pi32", "bfloat16": "pb16", "uint16": "pu16"}
+PLACE, SCRATCH = {}, {}
+_size = {k: 0 for k in POOL}
+for _k, _v in SB.items():
+    if _k in APART:
+        SCRATCH[_k] = ("sbuf", [128, _v[0]], _v[1])
+        PLACE[_k] = (_k, 0)
+    else:
+        PLACE[_k] = (POOL[_v[1]], _size[_v[1]])
+        _size[_v[1]] += (_v[0] + 31) // 32 * 32
+for _k, _v in POOL.items():
+    SCRATCH[_v] = ("sbuf", [128, _size[_k]], _k)
+PS = ["py", "pcn", "pu", "psc", "po", "ph", "pf", "pk"]
+for _p in PS:
+    SCRATCH[_p] = ("psum", [128, 512], "float32")
+ND = 10
+SEMAPHORES = ["qV", "qS", "qP", "qG", "loc"] + ["d%d" % i for i in range(ND)] + ["ak%d" % t for t in range(1, VI + 1)] + ["aa%d" % t for t in range(1, VI + 1)]
+
+
+def rank_program(g, core, T, topo):
+    rank = T.rank_of(core)
+    if rank is None:
+        return
+    cores = list(T.cores)
+    n = len(cores)
+    eng = {"V": g.vector, "S": g.scalar, "P": g.tensor, "G": g, "Y": g.sync}
+    cnt = {"V": 0, "S": 0, "P": 0, "G": 0}
+    known = {q: {} for q in eng}
+    snap = {}
+    wr, rd = {}, {}
+
+    def B(name, lo=0, hi=None, st=1):
+        if name in PS:
+            return (name, lo, 512 if hi is None else hi, st)
+        p, o = PLACE[name]
+        return (p, o + lo, o + (SB[name][0] if hi is None else hi), st)
+
+    def ap(v):
+        if v[0] == "I":
+            return ap(v[1]).indirect(ap(v[2]))
+        if v[3] == 1:
+            return T[v[0]][:, v[1]:v[2]]
+        return T[v[0]][:, v[1]:v[2]:v[3]]
+
+    def I(w, o):
+        return ("I", w, o)
+
+    def flat(vs):
+        out = []
+        for v in vs:
+            if v is None or isinstance(v, (int, float)):
+                continue
+            out += [v[1], v[2]] if v[0] == "I" else [v]
+        return out
+
+    def over(a, b):
+        if a[0] in PS:
+            return True
+        if a[1] >= b[2] or b[1] >= a[2]:
+            return False
+        return not (a[3] == b[3] and a[3] > 1 and (a[1] - b[1]) % a[3])
+
+    def need_wait(q, reads, writes):
+        need = {}
+
+        def add(rec, same_ok):
+            v, sem, val, rq = rec
+            if not (same_ok and rq == q) and known[q].get(sem, 0) < val:
+                need[sem] = max(need.get(sem, 0), val)
+        for r in reads:
+            for rec in wr.get(r[0], []):
+                if over(rec[0], r):
+                    add(rec, False)
+        for w in writes:
+            for rec in wr.get(w[0], []) + rd.get(w[0], []):
+                if over(rec[0], w):
+                    add(rec, q == "P")
+        for s in list(need):
+            for s2 in list(need):
+                if s2 != s and s in need and snap.get((s2, need[s2]), {}).get(s, 0) >= need[s]:
+                    del need[s]
+        for s, v in need.items():
+            eng[q].wait_ge(T.sem[s], v)
+            known[q][s] = v
+            for a, b in snap.get((s, v), {}).items():
+                known[q][a] = max(known[q].get(a, 0), b)
+
+    def record(q, reads, writes, sem, val):
+        snap[(sem, val)] = dict(known[q])
+        for w in writes:
+            def covered(r):
+                return r[0][1] >= w[1] and r[0][2] <= w[2] and (w[3] == 1 or (r[0][3] == w[3] and (r[0][1] - w[1]) % w[3] == 0))
+            wr[w[0]] = [r for r in wr.get(w[0], []) if not covered(r)] + [(w, sem, val, q)]
+            rd[w[0]] = [r for r in rd.get(w[0], []) if not covered(r)]
+        for r in reads:
+            rd[r[0]] = [x for x in rd.get(r[0], []) if not (x[0] == r and x[3] == q and x[1] == sem)] + [(r, sem, val, q)]
+
+    def op(q, ins, reads, writes):
+        rs = flat(reads) + [w[2] for w in writes if w[0] == "I"]
+        ws = [w[1] if w[0] == "I" else w for w in writes]
+        need_wait(q, rs, ws)
+        cnt[q] += 1
+        ins().then_inc(T.sem["q" + q], 1)
+        record(q, rs, ws, "q" + q, cnt[q])
+
+    def s_(v):
+        return ap(v) if isinstance(v, tuple) else v
+
+    def cp(o, i):
+        op("V", lambda: g.vector.tensor_copy(ap(o), ap(i)), [i], [o])
+
+    def tt(o, a, b, f):
+        op("V", lambda: g.vector.tensor_tensor(ap(o), ap(a), ap(b), f), [a, b], [o])
+
+    def ts(o, a, s1, f1, s2=None, f2=None):
+        if f2 is None:
+            op("V", lambda: g.vector.tensor_scalar(ap(o), ap(a), s_(s1), None, f1), [a, s1], [o])
+        else:
+            op("V", lambda: g.vector.tensor_scalar(ap(o), ap(a), s_(s1), s_(s2), f1, f2), [a, s1, s2], [o])
+
+    def red(o, i, f):
+        op("V", lambda: g.vector.tensor_reduce(ap(o), ap(i), X.X, f), [i], [o])
+
+    def scan(o, a, b, init, f0, f1):
+        op("V", lambda: g.vector.tensor_tensor_scan(ap(o), ap(a), ap(b), init, f0, f1), [a, b], [o])
+
+    def ms(o, c):
+        op("V", lambda: g.vector.memset(ap(o), c), [], [o])
+
+    def act(o, i, f=F.Copy, bias=None, scale=None, acc=None):
+        kw = {}
+        if bias is not None:
+            kw["bias"] = s_(bias)
+        if scale is not None:
+            kw["scale"] = s_(scale)
+        if acc is not None:
+            kw["accum_out"] = ap(acc)
+        op("S", lambda: g.scalar.activation(ap(o), ap(i), f, **kw), [i, bias, scale], [o] + ([] if acc is None else [acc]))
+
+    def mm(o, l, r, start=True, stop=True):
+        op("P", lambda: g.tensor.matmul(ap(o), ap(l), ap(r), start, stop), [l, r], [o])
+
+    def iota(o, pat, base, cm):
+        kw = {} if SCRATCH[o[0]][2] == "int32" else {"allow_small_or_imprecise_dtypes": True}
+        op("G", lambda: g.iota(ap(o), pat, base, cm, **kw), [], [o])
+
+    nd = [0]
+
+    def dma(q, o, i, reads, writes):
+        need_wait(q, reads, writes)
+        s = "d%d" % nd[0]
+        nd[0] += 1
+        eng[q].dma_start(o, i).then_inc(T.sem[s], 16)
+        snap[(s, 16)] = dict(known[q])
+        for w in writes:
+            wr[w[0]] = wr.get(w[0], []) + [(w, s, 16, "dma")]
+        for r in reads:
+            rd[r[0]] = rd.get(r[0], []) + [(r, s, 16, "dma")]
+        return q, s
+
+    locs = [0]
+
+    def ways(a, b):
+        return topo.engines(a, b)[:8]
+
+    def send(dst, dbuf, sbuf, sem):
+        need_wait("G", [B(sbuf)], [])
+        es = ways(core, dst)
+        rid, pid = topo.addr(dst)[:2]
+        g.remote_dma(T[dbuf][:], T[sbuf][:], T.sem[sem], T.sem["loc"], pid=pid, routing_id=rid, dma_engine_mask=sum(1 << e for e in es))
+        locs[0] += len(es)
+
+    def landed(buf, src, sem):
+        v = len(ways(src, core))
+        wr[buf] = wr.get(buf, []) + [(B(buf), sem, v, "net")]
+        snap[(sem, v)] = {}
+
+    nxt, prv = cores[(rank + 1) % n], cores[(rank - 1) % n]
+
+    dma("Y", T.sgi[:], T.sg0[:], [], [B("sgi")])
+    dma("S", T.trus[:], T.tru[:], [], [B("trus")])
+    dma("Y", T.kmi[:], T.km0[:], [], [B("kmi")])
+    dma("Y", ap(B("bk", 0, 2048)), T.book[:], [], [B("bk", 0, 2048)])
+    dma("S", ap(B("bk", 2048, 2560)), T.book[:, 0:512], [], [B("bk", 2048, 2560)])
+    dma("Y", ap(B("wti", 0, 1)), T.wt[:], [], [B("wti", 0, 1)])
+
+    iota(B("pi", 0, 1), [[1, 1]], 0, 1)
+    iota(B("iot", 0, 512), [[1, 512]], 0, 0)
+    iota(B("vs"), [[64, 8], [1, 16]], 0, 0)
+    iota(B("g8"), [[64, 8]], 0, 0)
+    iota(B("idt"), [[1, 128]], 0, -1)
+    iota(B("r16"), [[0, 8], [1, 16]], 0, 0)
+    iota(B("gi"), [[64, 8], [0, 16]], 0, 0)
+    iota(B("w68t"), [[-1024, 17], [-256, 4]], CB - 15, 0)
+    iota(B("j16t"), [[1, 64]], 0, 0)
+    iota(B("it8"), [[1, 8]], 0, 0)
+    iota(B("dut"), [[16, 16]], 4096, 0)
+    for w in (512, 1024, 2048):
+        act(B("iot", w, 2 * w), B("iot", 0, w), F.Identity, bias=float(w))
+    ms(B("selc"), 0.0)
+    ms(B("rst"), 0.0)
+    ms(B("rst", 0, 4096, 16), 512.0)
+    ts(B("pq", 0, 1), B("pi", 0, 1), 15, A.bitwise_and)
+    ts(B("pq", 1, 2), B("pi", 0, 1), 4, A.arith_shift_right)
+    ts(B("pq", 2, 3), B("pi", 0, 1), 3, A.bitwise_and)
+    ms(B("z", 4096, 4352), 0.0)
+    cp(B("pc", 0, 3), B("pq", 0, 3))
+    cp(B("sl"), B("sgi"))
+    q_, grp, q4 = B("pc", 0, 1), B("pc", 3, 4), B("pc", 2, 3)
+    ts(B("pc", 3, 4), B("pc", 1, 2), 64.0, A.mult)
+    ts(B("pc", 4, 5), B("pc", 0, 1), -16.0, A.mult)
+    ts(B("pc", 5, 6), B("pc", 0, 1), 64.0, A.mult)
+    for w in range(4):
+        ts(B("pc", 9 + w, 10 + w), B("pc", 0, 1), 4.0, A.mult, float(w), A.add)
+    tt(B("pc", 7, 8), B("pc", 3, 4), B("pc", 0, 1), A.subtract)
+    ts(B("pc", 8, 9), B("pc", 7, 8), 15.0, A.add)
+    ts(B("rev"), B("vs"), B("pc", 8, 9), A.is_equal)
+    cp(B("kmf"), B("kmi"))
+    for r in range(4):
+        cp(B("kf", r, 64, 4), B("kmf", 3 - r, 64, 4))
+    mm(B("pk", 0, 64), B("rev"), B("kf"))
+    cp(B("k16_0"), B("pk", 0, 64))
+    for q in range(16):
+        ts(B("selc", 128 * q + q, 128 * q + 128, 16), B("g8"), grp, A.is_equal, 65536.0, A.mult)
+    ts(B("idb"), B("idt"), 0.0, A.is_equal)
+    ms(B("cb"), -4352.0)
+    ms(B("on"), 1.0)
+    ms(B("lt", 0, 64), 0.0)
+    ms(B("scn", 16384, 17408), 0.0)
+    ts(B("sels"), B("selc"), 1.0 / 64, A.mult)
+    ts(B("gbf"), B("gi"), grp, A.is_equal)
+    cp(B("wtf", 0, 1), B("wti", 0, 1))
+    ts(B("wb"), B("gbf"), B("wtf", 0, 1), A.mult)
+    ts(B("mk"), B("r16"), q_, A.is_equal)
+    ts(B("ra"), B("r16"), 0.5, A.is_gt)
+    ts(B("rep4"), B("it8"), 0.0, A.mult, q4, A.add)
+    ts(B("w68"), B("w68t"), B("pc", 4, 5), A.add)
+    for h in range(2):
+        act(B("stab", 1024 * h, 1024 * h + 1024), I(B("iot"), B("sl", 64 * h, 64 * h + 64)))
+    act(B("z", 0, 2048), I(B("trus"), B("sl", 0, 128)))
+    cp(B("z", 2048, 4096), I(B("trus"), B("sl", 128, 256)))
+
+    def consts():
+        cp(B("w128", 0, 64), B("w68", 0, 64))
+        cp(B("w128", 64, 128), B("w68", 0, 64))
+        cp(B("val", 64, 68), B("w68", 64, 68))
+        ms(B("cc", 0, 1), 0.0)
+        ms(B("ab0"), 0.0)
+        ms(B("old0"), 0.0)
+        ms(B("stab", 4096, 4352), 0.0)
+        cp(B("rep16"), B("it8"))
+        ts(B("rw4"), B("it8"), 4.0, A.is_ge, 4.0, A.mult)
+        ts(B("j16"), B("j16t"), B("pc", 5, 6), A.add)
+        ts(B("rk2"), B("r16"), 0.0, A.is_equal, 2.0e9, A.mult)
+        ts(B("repw"), B("rw4"), q4, A.add)
+        ts(B("rk"), B("rk2"), -1.0e9, A.add)
+        ts(B("dum"), B("dut"), q_, A.add)
+        ms(B("msk"), 0.0)
+        ts(B("dm1"), B("dum", 8, 16), 2.0, A.add)
+        ms(B("own1"), 0.0)
+        ms(B("nh"), 0.0)
+        for r in range(4):
+            for w in range(4):
+                b = NB[r] + w * RW[r]
+                ts(B("msk", b, b + 64), B("j16t"), B("pc", 9 + w, 10 + w), A.is_le)
+
+    def ttg(a, b, t):
+        cp(B("tt", 64 * a, 64 * b), I(B("bk"), B("k16_%d" % t, 4 * a, 4 * b)))
+
+    def gat(a, b, q):
+        o, i = B("gg", 1024 * a, 1024 * b), I(B("z"), B("tt", 64 * a, 64 * b))
+        if q == "S":
+            act(o, i)
+        else:
+            cp(o, i)
+
+    def mins(a, b):
+        scan(B("scn", 1024 * a, 1024 * b), B("rst", 0, 1024 * (b - a)), B("gg", 1024 * a, 1024 * b), 512.0, A.max, A.min)
+
+    def less(a, b):
+        a = max(a, 1)
+        tt(B("lt", 64 * a, 64 * b), B("scn", 1024 * a + 15, 1024 * b, 16), B("py", 0, 64 * (b - a)), A.is_lt)
+
+    def abup(t, o):
+        tt(B("ad"), I(B("nw", 0, 8), B("repw")), B("ab%d" % t), A.subtract)
+        tt(B("ad2"), B("ad"), B("ohk"), A.mult)
+        tt(B(o), B("ab%d" % t), B("ad2"), A.add)
+
+    def st_gather(t):
+        act(B("sg2"), I(B("stab"), B("src%d" % t)))
+
+    def st_scatter(t):
+        cp(I(B("stab"), B("dst%d" % t)), B("sg2"))
+
+    thr = CB - 16390.0
+    ttg(0, 2, 0)
+    for t in range(VI):
+        last = t == VI - 1
+        K = "k16_%d" % t
+        gat(0, 2, "S")
+        ttg(2, 5, t)
+        gat(2, 5, "S")
+        ttg(12, 14, t)
+        if t:
+            abup(t - 1, "abs%d" % (t - 1))
+            send(nxt, "ab%d" % t, "abs%d" % (t - 1), "aa%d" % t)
+            landed("ab%d" % t, prv, "aa%d" % t)
+        gat(12, 14, "V")
+        ttg(5, 8, t)
+        gat(5, 8, "S")
+        mins(0, 2)
+        for k in range(4):
+            mm(B("py", 64 * k, 64 * k + 64), B("idb"), B("scn", 15, 1024, 16))
+        mm(B("pcn", 0, 64), B("cb"), B("on", 0, 64), True, False)
+        mins(12, 14)
+        ttg(8, 12, t)
+        gat(8, 11, "S")
+        gat(11, 12, "S")
+        ttg(14, 16, t)
+        if t == 0:
+            consts()
+        less(0, 2)
+        less(12, 14)
+        gat(14, 16, "V")
+        cp(B("kf"), B(K))
+        mins(2, 5)
+        mins(14, 16)
+        less(2, 5)
+        less(14, 16)
+        mins(5, 8)
+        less(5, 8)
+        mins(8, 11)
+        less(8, 11)
+        mins(11, 12)
+        less(11, 12)
+        act(B("scn", 16384 + 15, 17408, 16), B("scn", 1024 * (1 + t) + 15, 1024 * (2 + t), 16))
+        if t:
+            st_gather(t - 1)
+        else:
+            act(B("stab", 2048, 3072), I(B("iot"), B("sl", 128, 192)))
+        for q in range(16):
+            mm(B("pcn", 0, 64), B("selc", 128 * q, 128 * q + 128), B("lt", q, 1024, 16), False, q == 15)
+        if t:
+            st_scatter(t - 1)
+        tt(B("val", 0, 64), B("pcn", 0, 64), B("w68", 0, 64), A.min)
+        for r in range(4):
+            red(B("m", r, r + 1), B("val", r, 68, 4), A.max)
+        ts(B("off"), B("m", 0, 4), -1.0, A.mult, float(CB), A.add)
+        ts(B("nh", 0, 4), B("m", 0, 4), thr, A.is_lt, 16384.0 - 1024.0 * (1 + t), A.mult)
+        cp(B("ysel"), I(B("scn"), B("off")))
+        mm(B("pu", 0, 64), B("wb"), B("ysel"))
+        tt(B("m2", 0, 4), B("m", 0, 4), B("nh", 0, 4), A.add)
+        ts(B("hit", 0, 4), B("m", 0, 4), thr, A.is_ge)
+        tt(B("um"), B("pu", 0, 64), B("mk", 0, 64), A.mult)
+        tt(B("ohk"), I(B("m2", 0, 4), B("rep4")), B("w128"), A.is_equal)
+        scan(B("us"), B("ra", 0, 64), B("um"), 0.0, A.mult, A.add)
+        cp(B("ui", 0, 4), B("us", 15, 64, 16))
+        ts(B("ua", 0, 4), B("ui", 0, 4), 4095, A.bitwise_and)
+        tt(B("pr"), B("ab%d" % t), B("ohk"), A.mult)
+        for c in range(8):
+            w, r = c // 4, c % 4
+            act(B("prj", 16 * c, 16 * c + 16), B("pr", 64 * w + r, 64 * w + 64, 4), acc=B("old0", c, c + 1))
+        ts(B("ux", 0, 4), B("ua", 0, 4), -2048.0, A.add)
+        ts(B("uy", 0, 4), B("ua", 0, 4), 3232.0, A.add)
+        tt(B("uz", 0, 4), B("ux", 0, 4), B("uy", 0, 4), A.mult)
+        ts(B("un", 0, 4), B("uz", 0, 4), 5, A.arith_shift_right, 2047, A.bitwise_and)
+        ts(B("nl", 0, 8, 2), B("un", 0, 4), B("cc", 0, 1), A.add)
+        ts(B("nf", 0, 4), B("un", 0, 4), B("cc", 0, 1), A.add)
+        for r in range(4):
+            cp(B("e2", r, 64, 4), I(B("bk"), B("nl", 2 * r, 2 * r + 1)))
+        for h in range(2):
+            act(B("zg", 512 + 256 * h, 768 + 256 * h), I(B("z"), B("e2", 32 + 16 * h, 48 + 16 * h)))
+            cp(B("zg", 256 * h, 256 * h + 256), I(B("z"), B("e2", 16 * h, 16 * h + 16)))
+        order = [0, 1, 2, 3, 8, 9, 10, 11, 4, 5, 6, 7, 12, 13, 14, 15]
+        for q in order:
+            mm(B("psc", 0, 64), B("sels", 128 * q, 128 * q + 128), B("zg", 64 * q, 64 * q + 64), q == 0, q == 15)
+        act(B("tr"), I(B("iot"), B("e2")))
+        tt(B("old"), I(B("hit", 0, 4), B("rep4", 0, 1)), B("old0"), A.mult)
+        tt(B("kd"), I(B("nf", 0, 4), B("rep4", 0, 4)), B("kf"), A.subtract)
+        tt(B("rr"), I(B("old", 0, 8), B("rep16")), B("mk"), A.mult)
+        mm(B("po", 0, 128), B("gbf"), B("rr"))
+        mm(B("ph", 0, 4), B("on"), B("hit", 0, 4))
+        tt(B("kab", 0, 64), B("j16"), B("psc", 0, 64), A.subtract)
+        tt(B("kab", 64, 128), B("j16"), B("psc", 0, 64), A.add)
+        tt(B("kd2"), B("kd"), B("ohk", 0, 64), A.mult)
+        for w in range(2):
+            act(B("oth", 2 + w, 256, 4), B("po", 64 * w, 64 * w + 64), F.Identity, bias=-2.0)
+        scan(B("kss"), B("rk"), B("kab"), 0.0, A.max, A.min)
+        tt(B("kd3" if not last else "kint"), B("kd2"), B("kf"), A.add)
+        cp(B("ki"), B("kss", 15, 128, 16))
+        ts(B("owo"), B("old", 0, 8), 1.0, A.max, -2.0, A.add)
+        ts(B("ka"), B("ki"), 1023, A.bitwise_and)
+        if not last:
+            cp(B("ks%d" % (t + 1)), B("kd3"))
+            send(nxt, "k16_%d" % (t + 1), "ks%d" % (t + 1), "ak%d" % (t + 1))
+            landed("k16_%d" % (t + 1), prv, "ak%d" % (t + 1))
+        else:
+            ts(B("kin2"), B("kint"), 2047, A.bitwise_and)
+        cp(B("ofn"), B("ka"))
+        ts(B("has"), B("old", 0, 8), 0.5, A.is_gt)
+        for w in range(2):
+            act(B("oth", w, 256, 4), I(B("tr"), B("ofn", 4 * w, 4 * w + 4)))
+        tt(B("om"), I(B("tr"), B("ofn")), B("mk"), A.mult)
+        tt(B("pdo", 0, 4), B("old", 4, 8), B("dm1", 0, 4), A.subtract)
+        scan(B("osn"), B("ra"), B("om"), 0.0, A.mult, A.add)
+
+        def own(w, r):
+            return B("osn", 64 * w + 16 * r + 15, 64 * w + 16 * r + 16) if w < 2 else B("owo", 4 * w - 8 + r, 4 * w - 7 + r)
+
+        def blk(w, r):
+            return B("ne", NB[r] + w * RW[r], NB[r] + (w + 1) * RW[r])
+        for r in range(4):
+            for w in (2, 3) if r >= 1 else (2, 3, 1):
+                act(blk(w, r), B("oth", 64 * r, 256), F.Square, bias=own(w, r), scale=-1.0)
+        tt(B("pdo", 4, 8), B("old", 0, 4), B("dm1", 4, 8), A.subtract)
+        cp(B("src%d" % t, 8, 16), B("owo"))
+        for r in range(4):
+            for w in (0, 1) if r >= 1 else (0,):
+                ts(blk(w, r), B("oth", 64 * r, 256), own(w, r), A.not_equal)
+            if r == 0:
+                cp(B("src%d" % t, 0, 8), B("osn", 15, 128, 16))
+                tt(B("pd", 8, 16), B("pdo"), B("has"), A.mult)
+        if not last:
+            act(B("zg2"), I(B("z"), B("src%d" % t)))
+        tt(B("pd", 0, 4), B("osn", 79, 128, 16), B("dum", 0, 4), A.subtract)
+        tt(B("pd", 4, 8), B("osn", 15, 64, 16), B("dum", 4, 8), A.subtract)
+        ts(B("own1", 0, 8), B("osn", 15, 128, 16), 2.0, A.add)
+        red(B("cc", 0, 1), B("ph", 0, 4), A.add)
+        for r in range(4):
+            R = RW[r]
+            scan(B("ns", NB[r], NB[r] + 4 * R), B("ne", NB[r], NB[r] + 4 * R), B("msk", NB[r], NB[r] + 4 * R), 1.0, A.min, A.max)
+        for r in range(4):
+            R = RW[r]
+            red(B("acc", r, r + 1), B("ns", NB[r] + R - 1, NB[r] + 4 * R, R), A.min)
+        if not last:
+            ttg(0, 2, t + 1)
+        tt(B("dv"), I(B("acc", 0, 4), B("rep4", 0, 1)), B("pd"), A.mult)
+        tt(B("nw"), I(B("acc", 0, 4), B("rep4", 0, 1)), B("own1"), A.mult)
+        tt(B("da"), B("dv"), B("dum"), A.add)
+        if last:
+            st_gather(t)
+        cp(B("dst%d" % t), B("da"))
+        if not last:
+            cp(I(B("z"), B("dst%d" % t)), B("zg2"))
+        if t == 0:
+            act(B("stab", 3072, 4096), I(B("iot"), B("sl", 192, 256)))
+
+    abup(VI - 1, "fa")
+    for r in range(4):
+        ts(B("abs5", r, 128, 4), B("fa", 3 - r, 128, 4), 1.0, A.max, -2.0, A.add)
+    mm(B("pf", 0, 128), B("rev"), B("abs5"))
+    cp(B("sna"), B("pf", 0, 128))
+    send(prv, "lna", "sna", "aa%d" % VI)
+    st_scatter(VI - 1)
+    for r in range(4):
+        cp(B("kd", r, 64, 4), B("kin2", 3 - r, 64, 4))
+    mm(B("pk", 0, 64), B("rev"), B("kd"))
+    cp(B("snk"), B("pk", 0, 64))
+    send(prv, "lnk", "snk", "ak%d" % VI)
+    landed("lnk", nxt, "ak%d" % VI)
+    landed("lna", nxt, "aa%d" % VI)
+    ends = [dma("Y", T.ys[:], T.stab[::16, 0:4096], [B("stab")], []),
+            dma("S", T.ya[:], ap(B("lna", 0, 64)), [B("lna")], []),
+            dma("S", T.yb[:], ap(B("lna", 64, 128)), [B("lna")], []),
+            dma("Y", T.yk[:], T.lnk[:], [B("lnk")], [])]
+    for q, s in ends:
+        eng[q].wait_ge(T.sem[s], 16)
+    g.wait_ge(T.sem["loc"], locs[0])
+    for q in cnt:
+        if known["Y"].get("q" + q, 0) < cnt[q]:
+            g.sync.wait_ge(T.sem["q" + q], cnt[q])

@@ -4,33 +4,36 @@ VI = 6
 CB = 17500
 RW = [256, 192, 128, 64]
 NB = [0, 1024, 1792, 2304]
+PAIR = [(6, 8, 10), (10, 12.5, 15)]
 
 SB = {
     "bk": (2560, "int32"), "trus": (4096, "bfloat16"), "sgi": (256, "int32"), "sl": (256, "uint16"), "kmi": (64, "int32"),
     "kmf": (64, "float32"), "wti": (8, "int32"), "wtf": (8, "float32"),
     "z": (4352, "bfloat16"), "stab": (4352, "float32"), "iot": (4096, "float32"),
     "gg": (16384, "bfloat16"), "scn": (17408, "bfloat16"), "rst": (4096, "bfloat16"),
-    "tt": (1024, "uint16"), "lt": (1024, "bfloat16"), "val": (68, "float32"), "m": (8, "float32"), "m2": (8, "float32"),
+    "tt": (1024, "uint16"), "ta0": (128, "uint16"), "tb0": (128, "uint16"), "ta1": (160, "uint16"), "tb1": (160, "uint16"),
+    "lt": (1024, "bfloat16"), "val": (68, "float32"), "m": (8, "float32"), "m2": (8, "float32"),
     "nh": (8, "float32"), "off": (4, "uint16"), "ysel": (64, "bfloat16"), "um": (64, "float32"), "us": (64, "float32"),
     "ui": (8, "int32"), "ua": (8, "int32"), "ux": (8, "float32"), "uy": (8, "float32"), "uz": (8, "int32"), "un": (8, "int32"),
     "nl": (8, "uint16"), "nf": (8, "float32"), "e2": (64, "uint16"), "zg": (1024, "bfloat16"), "tr": (1024, "float32"),
-    "ohk": (128, "float32"), "kf": (64, "float32"), "kd": (64, "float32"), "kd2": (64, "float32"), "kd3": (64, "float32"),
+    "ohk": (64, "float32"), "nfr": (64, "float32"), "nwr": (128, "float32"), "idf": (128, "float32"), "nid": (128, "float32"),
+    "kf": (64, "float32"), "kd": (64, "float32"), "kd2": (64, "float32"),
     "pr": (128, "float32"), "prj": (128, "float32"), "old0": (16, "float32"), "old": (16, "float32"), "owo": (8, "float32"),
-    "has": (8, "float32"), "rr": (128, "float32"),
+    "rr": (128, "float32"),
     "oth": (256, "float32"), "kab": (128, "float32"), "kss": (128, "float32"), "ki": (8, "int32"), "ka": (8, "int32"),
     "ofn": (8, "uint16"), "om": (128, "float32"), "osn": (128, "float32"), "ne": (2560, "bfloat16"), "ns": (2560, "bfloat16"),
-    "acc": (8, "float32"), "pd": (16, "float32"), "pdo": (8, "float32"), "dv": (16, "float32"), "da": (16, "float32"),
-    "zg2": (256, "bfloat16"), "sg2": (256, "float32"), "own1": (16, "float32"), "nw": (16, "float32"),
-    "ad": (128, "float32"), "ad2": (128, "float32"), "hit": (8, "bfloat16"), "cc": (8, "float32"),
+    "acc": (8, "float32"), "pd": (16, "float32"), "da": (16, "float32"),
+    "zg2": (256, "bfloat16"), "sg2": (256, "float32"), "nw": (16, "float32"),
+    "ad": (128, "float32"), "ad2": (128, "float32"), "hit": (8, "bfloat16"), "ccj": (8, "float32"), "cc": (8, "float32"),
     "snk": (64, "float32"), "sna": (128, "float32"), "lnk": (64, "float32"), "lna": (128, "float32"),
-    "kint": (64, "int32"), "kin2": (64, "int32"), "fa": (128, "float32"),
+    "kint": (64, "int32"), "kin2": (64, "int32"), "fa": (128, "float32"), "fn": (128, "float32"),
     "pi": (8, "int32"), "pq": (8, "int32"), "pc": (16, "float32"), "selc": (2048, "bfloat16"),
     "sels": (2048, "bfloat16"), "gi": (128, "float32"), "g8": (8, "float32"), "gbf": (128, "float32"), "wb": (128, "bfloat16"),
     "idt": (128, "float32"), "idb": (128, "bfloat16"), "vs": (128, "float32"), "rev": (128, "float32"), "r16": (128, "float32"),
-    "mk": (128, "float32"), "w68t": (68, "float32"), "w68": (68, "float32"), "w128": (128, "float32"), "j16t": (64, "float32"),
+    "mk": (128, "float32"), "w68t": (68, "float32"), "w68": (68, "float32"), "j16t": (64, "float32"),
     "j16": (64, "float32"), "rk2": (128, "float32"), "rk": (128, "float32"), "ra": (128, "float32"), "rep4": (8, "uint16"),
     "rep16": (8, "uint16"), "repw": (8, "uint16"), "it8": (8, "float32"), "rw4": (8, "float32"), "msk": (2560, "bfloat16"),
-    "dut": (16, "float32"), "dum": (16, "float32"), "dm1": (8, "float32"), "cb": (128, "bfloat16"), "on": (128, "bfloat16"),
+    "dut": (16, "float32"), "dum": (16, "float32"), "cb": (128, "bfloat16"), "on": (128, "bfloat16"),
 }
 MSG = ["ab0"]
 for _t in range(VI + 1):
@@ -41,7 +44,7 @@ for _t in range(VI + 1):
     SB["ks%d" % _t] = (64, "uint16")
     SB["abs%d" % _t] = (128, "float32")
     MSG += ["k16_%d" % _t, "ab%d" % _t, "ks%d" % _t, "abs%d" % _t]
-APART = ["bk", "trus", "sgi", "kmi", "wti", "z", "stab", "iot", "gg", "scn", "rst", "lnk", "lna", "snk", "sna"] + MSG
+APART = ["bk", "trus", "sgi", "kmi", "wti", "z", "stab", "iot", "gg", "scn", "rst", "lnk", "lna", "snk", "sna", "ta0", "tb0", "ta1", "tb1"] + MSG
 POOL = {"float32": "pf32", "int32": "pi32", "bfloat16": "pb16", "uint16": "pu16"}
 PLACE, SCRATCH = {}, {}
 _size = {k: 0 for k in POOL}
@@ -57,7 +60,7 @@ for _k, _v in POOL.items():
 PS = ["py", "pcn", "pu", "psc", "po", "ph", "pf", "pk"]
 for _p in PS:
     SCRATCH[_p] = ("psum", [128, 512], "float32")
-ND = 10
+ND = 10 + 8 * VI
 SEMAPHORES = ["qV", "qS", "qP", "qG", "loc"] + ["d%d" % i for i in range(ND)] + ["ak%d" % t for t in range(1, VI + 1)] + ["aa%d" % t for t in range(1, VI + 1)]
 
 
@@ -190,8 +193,8 @@ def rank_program(g, core, T, topo):
 
     nd = [0]
 
-    def dma(q, o, i, reads, writes):
-        need_wait(q, reads, writes)
+    def dma(q, o, i, reads, writes, beside=False):
+        need_wait(q, reads, [] if beside else writes)
         s = "d%d" % nd[0]
         nd[0] += 1
         eng[q].dma_start(o, i).then_inc(T.sem[s], 16)
@@ -238,16 +241,24 @@ def rank_program(g, core, T, topo):
     iota(B("w68t"), [[-1024, 17], [-256, 4]], CB - 15, 0)
     iota(B("j16t"), [[1, 64]], 0, 0)
     iota(B("it8"), [[1, 8]], 0, 0)
-    iota(B("dut"), [[16, 16]], 4096, 0)
+    iota(B("dut"), [[16, 16]], -4096, 0)
+    for v in (B("msk"), B("stab", 4096, 4352), B("scn", 16384, 17408), B("scn", 6144, 16384, 2)):
+        iota(v, [[0, (v[2] - v[1]) // v[3]]], 0, 0)
     for w in (512, 1024, 2048):
         act(B("iot", w, 2 * w), B("iot", 0, w), F.Identity, bias=float(w))
     ms(B("selc"), 0.0)
+    ms(B("z", 4096, 4352), 0.0)
     ms(B("rst"), 0.0)
+    ms(B("cb"), -4352.0)
+    ms(B("on"), 1.0)
+    ms(B("lt", 0, 64), 0.0)
+    ms(B("cc", 0, 1), 0.0)
+    ms(B("ab0"), 0.0)
+    ms(B("old0"), 0.0)
     ms(B("rst", 0, 4096, 16), 512.0)
     ts(B("pq", 0, 1), B("pi", 0, 1), 15, A.bitwise_and)
     ts(B("pq", 1, 2), B("pi", 0, 1), 4, A.arith_shift_right)
     ts(B("pq", 2, 3), B("pi", 0, 1), 3, A.bitwise_and)
-    ms(B("z", 4096, 4352), 0.0)
     cp(B("pc", 0, 3), B("pq", 0, 3))
     cp(B("sl"), B("sgi"))
     q_, grp, q4 = B("pc", 0, 1), B("pc", 3, 4), B("pc", 2, 3)
@@ -267,10 +278,7 @@ def rank_program(g, core, T, topo):
     for q in range(16):
         ts(B("selc", 128 * q + q, 128 * q + 128, 16), B("g8"), grp, A.is_equal, 65536.0, A.mult)
     ts(B("idb"), B("idt"), 0.0, A.is_equal)
-    ms(B("cb"), -4352.0)
-    ms(B("on"), 1.0)
-    ms(B("lt", 0, 64), 0.0)
-    ms(B("scn", 16384, 17408), 0.0)
+    ts(B("idf"), B("idt"), 0.0, A.is_equal)
     ts(B("sels"), B("selc"), 1.0 / 64, A.mult)
     ts(B("gbf"), B("gi"), grp, A.is_equal)
     cp(B("wtf", 0, 1), B("wti", 0, 1))
@@ -279,19 +287,13 @@ def rank_program(g, core, T, topo):
     ts(B("ra"), B("r16"), 0.5, A.is_gt)
     ts(B("rep4"), B("it8"), 0.0, A.mult, q4, A.add)
     ts(B("w68"), B("w68t"), B("pc", 4, 5), A.add)
-    for h in range(2):
-        act(B("stab", 1024 * h, 1024 * h + 1024), I(B("iot"), B("sl", 64 * h, 64 * h + 64)))
-    act(B("z", 0, 2048), I(B("trus"), B("sl", 0, 128)))
-    cp(B("z", 2048, 4096), I(B("trus"), B("sl", 128, 256)))
+    act(B("stab", 0, 1024), I(B("iot"), B("sl", 0, 64)))
+    act(B("z", 0, 2560), I(B("trus"), B("sl", 0, 160)))
+    cp(B("z", 2560, 4096), I(B("trus"), B("sl", 160, 256)))
 
     def consts():
-        cp(B("w128", 0, 64), B("w68", 0, 64))
-        cp(B("w128", 64, 128), B("w68", 0, 64))
         cp(B("val", 64, 68), B("w68", 64, 68))
-        ms(B("cc", 0, 1), 0.0)
-        ms(B("ab0"), 0.0)
-        ms(B("old0"), 0.0)
-        ms(B("stab", 4096, 4352), 0.0)
+        ts(B("nid"), B("idf"), -1.0, A.mult)
         cp(B("rep16"), B("it8"))
         ts(B("rw4"), B("it8"), 4.0, A.is_ge, 4.0, A.mult)
         ts(B("j16"), B("j16t"), B("pc", 5, 6), A.add)
@@ -299,10 +301,6 @@ def rank_program(g, core, T, topo):
         ts(B("repw"), B("rw4"), q4, A.add)
         ts(B("rk"), B("rk2"), -1.0e9, A.add)
         ts(B("dum"), B("dut"), q_, A.add)
-        ms(B("msk"), 0.0)
-        ts(B("dm1"), B("dum", 8, 16), 2.0, A.add)
-        ms(B("own1"), 0.0)
-        ms(B("nh"), 0.0)
         for r in range(4):
             for w in range(4):
                 b = NB[r] + w * RW[r]
@@ -311,24 +309,40 @@ def rank_program(g, core, T, topo):
     def ttg(a, b, t):
         cp(B("tt", 64 * a, 64 * b), I(B("bk"), B("k16_%d" % t, 4 * a, 4 * b)))
 
-    def gat(a, b, q):
-        o, i = B("gg", 1024 * a, 1024 * b), I(B("z"), B("tt", 64 * a, 64 * b))
-        if q == "S":
-            act(o, i)
+    def swap(p):
+        lo, mid, hi = [int(64 * x) for x in PAIR[p]]
+        for d, par in (("ta%d" % p, 0), ("tb%d" % p, 1)):
+            for z, (a, b) in enumerate(((lo, mid), (mid, hi))):
+                v = B("tt", a, b)
+                dma("Y", T[d][z::2, :], T[v[0]][par::2, v[1]:v[2]], [v], [B(d)], z == 1)
+
+    def gat(p, a, b, q):
+        if p is None:
+            o, i = B("gg", 1024 * a, 1024 * b), I(B("z"), B("tt", 64 * a, 64 * b))
+            if q == "S":
+                act(o, i)
+            else:
+                cp(o, i)
         else:
-            cp(o, i)
+            o = 1024 * PAIR[p][0]
+            act(B("gg", o + 1024 * a, int(o + 1024 * b)), I(B("z"), B("ta%d" % p, 64 * a, int(64 * b))))
+
+    def fgat(p, a, b):
+        a, b = int(1024 * a), int(1024 * b)
+        o, m = 1024 * PAIR[p][0], int(1024 * PAIR[p][1])
+        tt(B("gg", m + a, m + b), I(B("z"), B("tb%d" % p, a // 16, b // 16)), B("gg", o + a, o + b), A.min)
 
     def mins(a, b):
         scan(B("scn", 1024 * a, 1024 * b), B("rst", 0, 1024 * (b - a)), B("gg", 1024 * a, 1024 * b), 512.0, A.max, A.min)
 
+    def pmins(p):
+        lo, mid, hi = [int(1024 * x) for x in PAIR[p]]
+        for z, a in ((0, lo), (1, mid)):
+            scan(B("scn", a + 1, a + mid - lo, 2), B("rst", 0, mid - lo, 2), B("gg", mid + z, hi, 2), 512.0, A.max, A.min)
+
     def less(a, b):
         a = max(a, 1)
         tt(B("lt", 64 * a, 64 * b), B("scn", 1024 * a + 15, 1024 * b, 16), B("py", 0, 64 * (b - a)), A.is_lt)
-
-    def abup(t, o):
-        tt(B("ad"), I(B("nw", 0, 8), B("repw")), B("ab%d" % t), A.subtract)
-        tt(B("ad2"), B("ad"), B("ohk"), A.mult)
-        tt(B(o), B("ab%d" % t), B("ad2"), A.add)
 
     def st_gather(t):
         act(B("sg2"), I(B("stab"), B("src%d" % t)))
@@ -337,53 +351,75 @@ def rank_program(g, core, T, topo):
         cp(I(B("stab"), B("dst%d" % t)), B("sg2"))
 
     thr = CB - 16390.0
-    ttg(0, 2, 0)
+    ttg(0, 1, 0)
     for t in range(VI):
         last = t == VI - 1
         K = "k16_%d" % t
-        gat(0, 2, "S")
-        ttg(2, 5, t)
-        gat(2, 5, "S")
-        ttg(12, 14, t)
+        ttg(1, 2, t)
+        ttg(6, 10, t)
+        swap(0)
+        gat(None, 0, 1, "S")
+        gat(None, 1, 2, "S")
+        ttg(2, 6, t)
+        gat(None, 5, 6, "V")
+        ttg(10, 14, t)
+        ttg(14, 16, t)
+        swap(1)
+        gat(0, 0, 1, "S")
         if t:
-            abup(t - 1, "abs%d" % (t - 1))
-            send(nxt, "ab%d" % t, "abs%d" % (t - 1), "aa%d" % t)
-            landed("ab%d" % t, prv, "aa%d" % t)
-        gat(12, 14, "V")
-        ttg(5, 8, t)
-        gat(5, 8, "S")
+            act(B("nwr"), I(B("nw", 0, 8), B("repw")))
+        gat(0, 1, 2, "S")
         mins(0, 2)
         for k in range(4):
             mm(B("py", 64 * k, 64 * k + 64), B("idb"), B("scn", 15, 1024, 16))
         mm(B("pcn", 0, 64), B("cb"), B("on", 0, 64), True, False)
-        mins(12, 14)
-        ttg(8, 12, t)
-        gat(8, 11, "S")
-        gat(11, 12, "S")
-        ttg(14, 16, t)
+        if t:
+            mm(B("pf", 0, 128), B("idf"), B("nwr"), True, False)
+            mm(B("pf", 0, 128), B("nid"), B("ab%d" % (t - 1)), False, True)
+        mins(5, 6)
+        fgat(0, 0, 1)
+        less(0, 2)
+        less(5, 6)
+        if t:
+            for w in range(2):
+                tt(B("ad2", 64 * w, 64 * w + 64), B("pf", 64 * w, 64 * w + 64), B("ohk"), A.mult)
+            mm(B("pf", 0, 128), B("idf"), B("ab%d" % (t - 1)), True, False)
+            mm(B("pf", 0, 128), B("idf"), B("ad2"), False, True)
+        gat(1, 0, 1, "S")
+        gat(1, 1, 2.5, "S")
+        if t:
+            act(B("abs%d" % (t - 1)), B("pf", 0, 128))
+            send(nxt, "ab%d" % t, "abs%d" % (t - 1), "aa%d" % t)
+            landed("ab%d" % t, prv, "aa%d" % t)
+        fgat(0, 1, 2)
+        pmins(0)
         if t == 0:
             consts()
-        less(0, 2)
-        less(12, 14)
-        gat(14, 16, "V")
+        less(6, 10)
+        fgat(1, 0, 1)
+        gat(None, 15, 16, "S")
+        gat(None, 2, 4, "S")
+        gat(None, 4, 5, "S")
+        fgat(1, 1, 2.5)
         cp(B("kf"), B(K))
-        mins(2, 5)
-        mins(14, 16)
-        less(2, 5)
-        less(14, 16)
-        mins(5, 8)
-        less(5, 8)
-        mins(8, 11)
-        less(8, 11)
-        mins(11, 12)
-        less(11, 12)
-        act(B("scn", 16384 + 15, 17408, 16), B("scn", 1024 * (1 + t) + 15, 1024 * (2 + t), 16))
+        pmins(1)
+        mm(B("pf", 0, 128), B("idf"), B("ab%d" % t))
+        mins(15, 16)
+        less(10, 13)
+        less(13, 16)
+        mins(2, 4)
+        less(2, 4)
+        mins(4, 5)
+        less(4, 5)
         if t:
             st_gather(t - 1)
-        else:
-            act(B("stab", 2048, 3072), I(B("iot"), B("sl", 128, 192)))
+        act(B("scn", 16384 + 15, 17408, 16), B("scn", 1024 * (1 + t) + 15, 1024 * (2 + t), 16))
+        if t == 0:
+            for h in (1, 2):
+                act(B("stab", 1024 * h, 1024 * h + 1024), I(B("iot"), B("sl", 64 * h, 64 * h + 64)))
         for q in range(16):
             mm(B("pcn", 0, 64), B("selc", 128 * q, 128 * q + 128), B("lt", q, 1024, 16), False, q == 15)
+        mm(B("py", 0, 64), B("idf"), B("kf"), True, False)
         if t:
             st_scatter(t - 1)
         tt(B("val", 0, 64), B("pcn", 0, 64), B("w68", 0, 64), A.min)
@@ -396,13 +432,14 @@ def rank_program(g, core, T, topo):
         tt(B("m2", 0, 4), B("m", 0, 4), B("nh", 0, 4), A.add)
         ts(B("hit", 0, 4), B("m", 0, 4), thr, A.is_ge)
         tt(B("um"), B("pu", 0, 64), B("mk", 0, 64), A.mult)
-        tt(B("ohk"), I(B("m2", 0, 4), B("rep4")), B("w128"), A.is_equal)
+        tt(B("ohk"), I(B("m2", 0, 4), B("rep4", 0, 4)), B("w68", 0, 64), A.is_equal)
         scan(B("us"), B("ra", 0, 64), B("um"), 0.0, A.mult, A.add)
         cp(B("ui", 0, 4), B("us", 15, 64, 16))
         ts(B("ua", 0, 4), B("ui", 0, 4), 4095, A.bitwise_and)
-        tt(B("pr"), B("ab%d" % t), B("ohk"), A.mult)
+        for w in range(2):
+            tt(B("pr", 64 * w, 64 * w + 64), B("pf", 64 * w, 64 * w + 64), B("ohk"), A.mult)
         for c in range(8):
-            w, r = c // 4, c % 4
+            w, r = 1 - c // 4, c % 4
             act(B("prj", 16 * c, 16 * c + 16), B("pr", 64 * w + r, 64 * w + 64, 4), acc=B("old0", c, c + 1))
         ts(B("ux", 0, 4), B("ua", 0, 4), -2048.0, A.add)
         ts(B("uy", 0, 4), B("ua", 0, 4), 3232.0, A.add)
@@ -410,6 +447,9 @@ def rank_program(g, core, T, topo):
         ts(B("un", 0, 4), B("uz", 0, 4), 5, A.arith_shift_right, 2047, A.bitwise_and)
         ts(B("nl", 0, 8, 2), B("un", 0, 4), B("cc", 0, 1), A.add)
         ts(B("nf", 0, 4), B("un", 0, 4), B("cc", 0, 1), A.add)
+        act(B("nfr"), I(B("nf", 0, 4), B("rep4", 0, 4)))
+        mm(B("pk", 0, 64), B("idf"), B("nfr"), True, False)
+        mm(B("pk", 0, 64), B("nid"), B("kf"), False, True)
         for r in range(4):
             cp(B("e2", r, 64, 4), I(B("bk"), B("nl", 2 * r, 2 * r + 1)))
         for h in range(2):
@@ -420,32 +460,31 @@ def rank_program(g, core, T, topo):
             mm(B("psc", 0, 64), B("sels", 128 * q, 128 * q + 128), B("zg", 64 * q, 64 * q + 64), q == 0, q == 15)
         act(B("tr"), I(B("iot"), B("e2")))
         tt(B("old"), I(B("hit", 0, 4), B("rep4", 0, 1)), B("old0"), A.mult)
-        tt(B("kd"), I(B("nf", 0, 4), B("rep4", 0, 4)), B("kf"), A.subtract)
+        tt(B("kd2"), B("pk", 0, 64), B("ohk"), A.mult)
         tt(B("rr"), I(B("old", 0, 8), B("rep16")), B("mk"), A.mult)
+        mm(B("py", 0, 64), B("idf"), B("kd2"), False, True)
         mm(B("po", 0, 128), B("gbf"), B("rr"))
         mm(B("ph", 0, 4), B("on"), B("hit", 0, 4))
-        tt(B("kab", 0, 64), B("j16"), B("psc", 0, 64), A.subtract)
-        tt(B("kab", 64, 128), B("j16"), B("psc", 0, 64), A.add)
-        tt(B("kd2"), B("kd"), B("ohk", 0, 64), A.mult)
+        tt(B("kab", 0, 64), B("j16"), B("psc", 0, 64), A.add)
+        tt(B("kab", 64, 128), B("j16"), B("psc", 0, 64), A.subtract)
         for w in range(2):
-            act(B("oth", 2 + w, 256, 4), B("po", 64 * w, 64 * w + 64), F.Identity, bias=-2.0)
+            act(B("oth", 2 + w, 256, 4), B("po", 64 * w, 64 * w + 64), F.Identity, bias=8192.0)
         scan(B("kss"), B("rk"), B("kab"), 0.0, A.max, A.min)
-        tt(B("kd3" if not last else "kint"), B("kd2"), B("kf"), A.add)
         cp(B("ki"), B("kss", 15, 128, 16))
-        ts(B("owo"), B("old", 0, 8), 1.0, A.max, -2.0, A.add)
+        ts(B("owo"), B("old", 0, 8), 8192.0, A.add, 4351.0, A.min)
         ts(B("ka"), B("ki"), 1023, A.bitwise_and)
         if not last:
-            cp(B("ks%d" % (t + 1)), B("kd3"))
+            cp(B("ks%d" % (t + 1)), B("py", 0, 64))
             send(nxt, "k16_%d" % (t + 1), "ks%d" % (t + 1), "ak%d" % (t + 1))
             landed("k16_%d" % (t + 1), prv, "ak%d" % (t + 1))
         else:
+            cp(B("kint"), B("py", 0, 64))
             ts(B("kin2"), B("kint"), 2047, A.bitwise_and)
         cp(B("ofn"), B("ka"))
-        ts(B("has"), B("old", 0, 8), 0.5, A.is_gt)
+        cp(B("src%d" % t, 8, 16), B("owo"))
         for w in range(2):
             act(B("oth", w, 256, 4), I(B("tr"), B("ofn", 4 * w, 4 * w + 4)))
         tt(B("om"), I(B("tr"), B("ofn")), B("mk"), A.mult)
-        tt(B("pdo", 0, 4), B("old", 4, 8), B("dm1", 0, 4), A.subtract)
         scan(B("osn"), B("ra"), B("om"), 0.0, A.mult, A.add)
 
         def own(w, r):
@@ -454,22 +493,19 @@ def rank_program(g, core, T, topo):
         def blk(w, r):
             return B("ne", NB[r] + w * RW[r], NB[r] + (w + 1) * RW[r])
         for r in range(4):
-            for w in (2, 3) if r >= 1 else (2, 3, 1):
+            for w in (2, 3) if r >= 2 else (2, 3, 1):
                 act(blk(w, r), B("oth", 64 * r, 256), F.Square, bias=own(w, r), scale=-1.0)
-        tt(B("pdo", 4, 8), B("old", 0, 4), B("dm1", 4, 8), A.subtract)
-        cp(B("src%d" % t, 8, 16), B("owo"))
         for r in range(4):
-            for w in (0, 1) if r >= 1 else (0,):
+            for w in (0, 1) if r >= 2 else (0,):
                 ts(blk(w, r), B("oth", 64 * r, 256), own(w, r), A.not_equal)
             if r == 0:
                 cp(B("src%d" % t, 0, 8), B("osn", 15, 128, 16))
-                tt(B("pd", 8, 16), B("pdo"), B("has"), A.mult)
         if not last:
             act(B("zg2"), I(B("z"), B("src%d" % t)))
-        tt(B("pd", 0, 4), B("osn", 79, 128, 16), B("dum", 0, 4), A.subtract)
-        tt(B("pd", 4, 8), B("osn", 15, 64, 16), B("dum", 4, 8), A.subtract)
-        ts(B("own1", 0, 8), B("osn", 15, 128, 16), 2.0, A.add)
-        red(B("cc", 0, 1), B("ph", 0, 4), A.add)
+        for w in range(2):
+            act(B("pd", 4 * w, 4 * w + 4), B("osn", 79 - 64 * w, 128 - 64 * w, 16), F.Identity, bias=-8192.0)
+            act(B("pd", 8 + 4 * w, 12 + 4 * w), B("old", 4 - 4 * w, 8 - 4 * w))
+        act(B("ccj", 0, 4), B("ph", 0, 4), acc=B("cc", 0, 1))
         for r in range(4):
             R = RW[r]
             scan(B("ns", NB[r], NB[r] + 4 * R), B("ne", NB[r], NB[r] + 4 * R), B("msk", NB[r], NB[r] + 4 * R), 1.0, A.min, A.max)
@@ -477,30 +513,34 @@ def rank_program(g, core, T, topo):
             R = RW[r]
             red(B("acc", r, r + 1), B("ns", NB[r] + R - 1, NB[r] + 4 * R, R), A.min)
         if not last:
-            ttg(0, 2, t + 1)
-        tt(B("dv"), I(B("acc", 0, 4), B("rep4", 0, 1)), B("pd"), A.mult)
-        tt(B("nw"), I(B("acc", 0, 4), B("rep4", 0, 1)), B("own1"), A.mult)
-        tt(B("da"), B("dv"), B("dum"), A.add)
+            ttg(0, 1, t + 1)
+        tt(B("nw"), I(B("acc", 0, 4), B("rep4", 0, 1)), B("pd"), A.mult)
+        tt(B("da"), B("nw"), B("dum"), A.min)
         if last:
             st_gather(t)
-        cp(B("dst%d" % t), B("da"))
+        ts(B("dst%d" % t), B("da"), 8192.0, A.add)
         if not last:
             cp(I(B("z"), B("dst%d" % t)), B("zg2"))
         if t == 0:
             act(B("stab", 3072, 4096), I(B("iot"), B("sl", 192, 256)))
 
-    abup(VI - 1, "fa")
-    for r in range(4):
-        ts(B("abs5", r, 128, 4), B("fa", 3 - r, 128, 4), 1.0, A.max, -2.0, A.add)
-    mm(B("pf", 0, 128), B("rev"), B("abs5"))
-    cp(B("sna"), B("pf", 0, 128))
-    send(prv, "lna", "sna", "aa%d" % VI)
-    st_scatter(VI - 1)
+    o = "ab%d" % (VI - 1)
+    tt(B("ad"), I(B("nw", 0, 8), B("repw")), B(o), A.subtract)
+    for w in range(2):
+        tt(B("ad2", 64 * w, 64 * w + 64), B("ad", 64 * w, 64 * w + 64), B("ohk"), A.mult)
+    tt(B("fa"), B(o), B("ad2"), A.add)
+    ts(B("fn"), B("fa"), 0.0, A.is_equal, -8193.0, A.mult)
+    mm(B("pf", 0, 128), B("rev"), B("fa"), True, False)
+    mm(B("pf", 0, 128), B("rev"), B("fn"), False, True)
     for r in range(4):
         cp(B("kd", r, 64, 4), B("kin2", 3 - r, 64, 4))
     mm(B("pk", 0, 64), B("rev"), B("kd"))
+    for r in range(4):
+        ts(B("sna", r, 128, 4), B("pf", 3 - r, 128, 4), 8192.0, A.add)
+    send(prv, "lna", "sna", "aa%d" % VI)
     cp(B("snk"), B("pk", 0, 64))
     send(prv, "lnk", "snk", "ak%d" % VI)
+    st_scatter(VI - 1)
     landed("lnk", nxt, "ak%d" % VI)
     landed("lna", nxt, "aa%d" % VI)
     ends = [dma("Y", T.ys[:], T.stab[::16, 0:4096], [B("stab")], []),

from concourse.mybir import AluOpType as A, AxisListType as X, ActivationFunctionType as F

VI = 6
CB = 17500
RW = [256, 192, 128, 64]
NB = [0, 1024, 1792, 2304]
PAIR = [(6, 8, 10), (10, 12.5, 15)]

SB = {
    "bk": (2560, "int32"), "trus": (4096, "bfloat16"), "sgi": (256, "int32"), "sl": (256, "uint16"), "kmi": (64, "int32"),
    "kmf": (64, "float32"), "wti": (8, "int32"), "wtf": (8, "float32"),
    "z": (4352, "bfloat16"), "stab": (4352, "float32"), "iot": (4096, "float32"),
    "gg": (16384, "bfloat16"), "scn": (17408, "bfloat16"), "rst": (4096, "bfloat16"),
    "tt": (1024, "uint16"), "ta0": (128, "uint16"), "tb0": (128, "uint16"), "ta1": (160, "uint16"), "tb1": (160, "uint16"),
    "lt": (1024, "bfloat16"), "val": (68, "float32"), "m": (8, "float32"), "m2": (8, "float32"),
    "nh": (8, "float32"), "off": (4, "uint16"), "ysel": (64, "bfloat16"), "um": (64, "float32"), "us": (64, "float32"),
    "ui": (8, "int32"), "ua": (8, "int32"), "ux": (8, "float32"), "uy": (8, "float32"), "uz": (8, "int32"), "un": (8, "int32"),
    "nl": (8, "uint16"), "nf": (8, "float32"), "e2": (64, "uint16"), "zg": (1024, "bfloat16"), "tr": (1024, "float32"),
    "ohk": (64, "float32"), "nfr": (64, "float32"), "nwr": (128, "float32"), "idf": (128, "float32"), "nid": (128, "float32"),
    "kf": (64, "float32"), "kd": (64, "float32"), "kd2": (64, "float32"),
    "pr": (128, "float32"), "prj": (128, "float32"), "old0": (16, "float32"), "old": (16, "float32"), "owo": (8, "float32"),
    "rr": (128, "float32"),
    "oth": (256, "float32"), "kab": (128, "float32"), "kss": (128, "float32"), "ki": (8, "int32"), "ka": (8, "int32"),
    "ofn": (8, "uint16"), "om": (128, "float32"), "osn": (128, "float32"), "ne": (2560, "bfloat16"), "ns": (2560, "bfloat16"),
    "acc": (8, "float32"), "pd": (16, "float32"), "da": (16, "float32"),
    "zg2": (256, "bfloat16"), "sg2": (256, "float32"), "nw": (16, "float32"),
    "ad": (128, "float32"), "ad2": (128, "float32"), "hit": (8, "bfloat16"), "ccj": (8, "float32"), "cc": (8, "float32"),
    "snk": (64, "float32"), "sna": (128, "float32"), "lnk": (64, "float32"), "lna": (128, "float32"),
    "kint": (64, "int32"), "kin2": (64, "int32"), "fa": (128, "float32"), "fn": (128, "float32"),
    "pi": (8, "int32"), "pq": (8, "int32"), "pc": (16, "float32"), "selc": (2048, "bfloat16"),
    "sels": (2048, "bfloat16"), "gi": (128, "float32"), "g8": (8, "float32"), "gbf": (128, "float32"), "wb": (128, "bfloat16"),
    "idt": (128, "float32"), "idb": (128, "bfloat16"), "vs": (128, "float32"), "rev": (128, "float32"), "r16": (128, "float32"),
    "mk": (128, "float32"), "w68t": (68, "float32"), "w68": (68, "float32"), "j16t": (64, "float32"),
    "j16": (64, "float32"), "rk2": (128, "float32"), "rk": (128, "float32"), "ra": (128, "float32"), "rep4": (8, "uint16"),
    "rep16": (8, "uint16"), "repw": (8, "uint16"), "it8": (8, "float32"), "rw4": (8, "float32"), "msk": (2560, "bfloat16"),
    "dut": (16, "float32"), "dum": (16, "float32"), "cb": (128, "bfloat16"), "on": (128, "bfloat16"),
}
MSG = ["ab0"]
for _t in range(VI + 1):
    SB["k16_%d" % _t] = (64, "uint16")
    SB["src%d" % _t] = (16, "uint16")
    SB["dst%d" % _t] = (16, "uint16")
    SB["ab%d" % _t] = (128, "float32")
    SB["ks%d" % _t] = (64, "uint16")
    SB["abs%d" % _t] = (128, "float32")
    MSG += ["k16_%d" % _t, "ab%d" % _t, "ks%d" % _t, "abs%d" % _t]
APART = ["bk", "trus", "sgi", "kmi", "wti", "z", "stab", "iot", "gg", "scn", "rst", "lnk", "lna", "snk", "sna", "ta0", "tb0", "ta1", "tb1"] + MSG
POOL = {"float32": "pf32", "int32": "pi32", "bfloat16": "pb16", "uint16": "pu16"}
PLACE, SCRATCH = {}, {}
_size = {k: 0 for k in POOL}
for _k, _v in SB.items():
    if _k in APART:
        SCRATCH[_k] = ("sbuf", [128, _v[0]], _v[1])
        PLACE[_k] = (_k, 0)
    else:
        PLACE[_k] = (POOL[_v[1]], _size[_v[1]])
        _size[_v[1]] += (_v[0] + 31) // 32 * 32
for _k, _v in POOL.items():
    SCRATCH[_v] = ("sbuf", [128, _size[_k]], _k)
PS = ["py", "pcn", "pu", "psc", "po", "ph", "pf", "pk"]
for _p in PS:
    SCRATCH[_p] = ("psum", [128, 512], "float32")
ND = 10 + 8 * VI
SEMAPHORES = ["qV", "qS", "qP", "qG", "loc"] + ["d%d" % i for i in range(ND)] + ["ak%d" % t for t in range(1, VI + 1)] + ["aa%d" % t for t in range(1, VI + 1)]


def rank_program(g, core, T, topo):
    rank = T.rank_of(core)
    if rank is None:
        return
    cores = list(T.cores)
    n = len(cores)
    eng = {"V": g.vector, "S": g.scalar, "P": g.tensor, "G": g, "Y": g.sync}
    cnt = {"V": 0, "S": 0, "P": 0, "G": 0}
    known = {q: {} for q in eng}
    snap = {}
    wr, rd = {}, {}

    def B(name, lo=0, hi=None, st=1):
        if name in PS:
            return (name, lo, 512 if hi is None else hi, st)
        p, o = PLACE[name]
        return (p, o + lo, o + (SB[name][0] if hi is None else hi), st)

    def ap(v):
        if v[0] == "I":
            return ap(v[1]).indirect(ap(v[2]))
        if v[3] == 1:
            return T[v[0]][:, v[1]:v[2]]
        return T[v[0]][:, v[1]:v[2]:v[3]]

    def I(w, o):
        return ("I", w, o)

    def flat(vs):
        out = []
        for v in vs:
            if v is None or isinstance(v, (int, float)):
                continue
            out += [v[1], v[2]] if v[0] == "I" else [v]
        return out

    def over(a, b):
        if a[0] in PS:
            return True
        if a[1] >= b[2] or b[1] >= a[2]:
            return False
        return not (a[3] == b[3] and a[3] > 1 and (a[1] - b[1]) % a[3])

    def need_wait(q, reads, writes):
        need = {}

        def add(rec, same_ok):
            v, sem, val, rq = rec
            if not (same_ok and rq == q) and known[q].get(sem, 0) < val:
                need[sem] = max(need.get(sem, 0), val)
        for r in reads:
            for rec in wr.get(r[0], []):
                if over(rec[0], r):
                    add(rec, False)
        for w in writes:
            for rec in wr.get(w[0], []) + rd.get(w[0], []):
                if over(rec[0], w):
                    add(rec, q == "P")
        for s in list(need):
            for s2 in list(need):
                if s2 != s and s in need and snap.get((s2, need[s2]), {}).get(s, 0) >= need[s]:
                    del need[s]
        for s, v in need.items():
            eng[q].wait_ge(T.sem[s], v)
            known[q][s] = v
            for a, b in snap.get((s, v), {}).items():
                known[q][a] = max(known[q].get(a, 0), b)

    def record(q, reads, writes, sem, val):
        snap[(sem, val)] = dict(known[q])
        for w in writes:
            def covered(r):
                return r[0][1] >= w[1] and r[0][2] <= w[2] and (w[3] == 1 or (r[0][3] == w[3] and (r[0][1] - w[1]) % w[3] == 0))
            wr[w[0]] = [r for r in wr.get(w[0], []) if not covered(r)] + [(w, sem, val, q)]
            rd[w[0]] = [r for r in rd.get(w[0], []) if not covered(r)]
        for r in reads:
            rd[r[0]] = [x for x in rd.get(r[0], []) if not (x[0] == r and x[3] == q and x[1] == sem)] + [(r, sem, val, q)]

    def op(q, ins, reads, writes):
        rs = flat(reads) + [w[2] for w in writes if w[0] == "I"]
        ws = [w[1] if w[0] == "I" else w for w in writes]
        need_wait(q, rs, ws)
        cnt[q] += 1
        ins().then_inc(T.sem["q" + q], 1)
        record(q, rs, ws, "q" + q, cnt[q])

    def s_(v):
        return ap(v) if isinstance(v, tuple) else v

    def cp(o, i):
        op("V", lambda: g.vector.tensor_copy(ap(o), ap(i)), [i], [o])

    def tt(o, a, b, f):
        op("V", lambda: g.vector.tensor_tensor(ap(o), ap(a), ap(b), f), [a, b], [o])

    def ts(o, a, s1, f1, s2=None, f2=None):
        if f2 is None:
            op("V", lambda: g.vector.tensor_scalar(ap(o), ap(a), s_(s1), None, f1), [a, s1], [o])
        else:
            op("V", lambda: g.vector.tensor_scalar(ap(o), ap(a), s_(s1), s_(s2), f1, f2), [a, s1, s2], [o])

    def red(o, i, f):
        op("V", lambda: g.vector.tensor_reduce(ap(o), ap(i), X.X, f), [i], [o])

    def scan(o, a, b, init, f0, f1):
        op("V", lambda: g.vector.tensor_tensor_scan(ap(o), ap(a), ap(b), init, f0, f1), [a, b], [o])

    def ms(o, c):
        op("V", lambda: g.vector.memset(ap(o), c), [], [o])

    def act(o, i, f=F.Copy, bias=None, scale=None, acc=None):
        kw = {}
        if bias is not None:
            kw["bias"] = s_(bias)
        if scale is not None:
            kw["scale"] = s_(scale)
        if acc is not None:
            kw["accum_out"] = ap(acc)
        op("S", lambda: g.scalar.activation(ap(o), ap(i), f, **kw), [i, bias, scale], [o] + ([] if acc is None else [acc]))

    def mm(o, l, r, start=True, stop=True):
        op("P", lambda: g.tensor.matmul(ap(o), ap(l), ap(r), start, stop), [l, r], [o])

    def iota(o, pat, base, cm):
        kw = {} if SCRATCH[o[0]][2] == "int32" else {"allow_small_or_imprecise_dtypes": True}
        op("G", lambda: g.iota(ap(o), pat, base, cm, **kw), [], [o])

    nd = [0]

    def dma(q, o, i, reads, writes, beside=False):
        need_wait(q, reads, [] if beside else writes)
        s = "d%d" % nd[0]
        nd[0] += 1
        eng[q].dma_start(o, i).then_inc(T.sem[s], 16)
        snap[(s, 16)] = dict(known[q])
        for w in writes:
            wr[w[0]] = wr.get(w[0], []) + [(w, s, 16, "dma")]
        for r in reads:
            rd[r[0]] = rd.get(r[0], []) + [(r, s, 16, "dma")]
        return q, s

    locs = [0]

    def ways(a, b):
        return topo.engines(a, b)[:8]

    def send(dst, dbuf, sbuf, sem):
        need_wait("G", [B(sbuf)], [])
        es = ways(core, dst)
        rid, pid = topo.addr(dst)[:2]
        g.remote_dma(T[dbuf][:], T[sbuf][:], T.sem[sem], T.sem["loc"], pid=pid, routing_id=rid, dma_engine_mask=sum(1 << e for e in es))
        locs[0] += len(es)

    def landed(buf, src, sem):
        v = len(ways(src, core))
        wr[buf] = wr.get(buf, []) + [(B(buf), sem, v, "net")]
        snap[(sem, v)] = {}

    nxt, prv = cores[(rank + 1) % n], cores[(rank - 1) % n]

    dma("Y", T.sgi[:], T.sg0[:], [], [B("sgi")])
    dma("S", T.trus[:], T.tru[:], [], [B("trus")])
    dma("Y", T.kmi[:], T.km0[:], [], [B("kmi")])
    dma("Y", ap(B("bk", 0, 2048)), T.book[:], [], [B("bk", 0, 2048)])
    dma("S", ap(B("bk", 2048, 2560)), T.book[:, 0:512], [], [B("bk", 2048, 2560)])
    dma("Y", ap(B("wti", 0, 1)), T.wt[:], [], [B("wti", 0, 1)])

    iota(B("pi", 0, 1), [[1, 1]], 0, 1)
    iota(B("iot", 0, 512), [[1, 512]], 0, 0)
    iota(B("vs"), [[64, 8], [1, 16]], 0, 0)
    iota(B("g8"), [[64, 8]], 0, 0)
    iota(B("idt"), [[1, 128]], 0, -1)
    iota(B("r16"), [[0, 8], [1, 16]], 0, 0)
    iota(B("gi"), [[64, 8], [0, 16]], 0, 0)
    iota(B("w68t"), [[-1024, 17], [-256, 4]], CB - 15, 0)
    iota(B("j16t"), [[1, 64]], 0, 0)
    iota(B("it8"), [[1, 8]], 0, 0)
    iota(B("dut"), [[16, 16]], -4096, 0)
    for v in (B("msk"), B("stab", 4096, 4352), B("scn", 16384, 17408), B("scn", 6144, 16384, 2)):
        iota(v, [[0, (v[2] - v[1]) // v[3]]], 0, 0)
    for w in (512, 1024, 2048):
        act(B("iot", w, 2 * w), B("iot", 0, w), F.Identity, bias=float(w))
    ms(B("selc"), 0.0)
    ms(B("z", 4096, 4352), 0.0)
    ms(B("rst"), 0.0)
    ms(B("cb"), -4352.0)
    ms(B("on"), 1.0)
    ms(B("lt", 0, 64), 0.0)
    ms(B("cc", 0, 1), 0.0)
    ms(B("ab0"), 0.0)
    ms(B("old0"), 0.0)
    ms(B("rst", 0, 4096, 16), 512.0)
    ts(B("pq", 0, 1), B("pi", 0, 1), 15, A.bitwise_and)
    ts(B("pq", 1, 2), B("pi", 0, 1), 4, A.arith_shift_right)
    ts(B("pq", 2, 3), B("pi", 0, 1), 3, A.bitwise_and)
    cp(B("pc", 0, 3), B("pq", 0, 3))
    cp(B("sl"), B("sgi"))
    q_, grp, q4 = B("pc", 0, 1), B("pc", 3, 4), B("pc", 2, 3)
    ts(B("pc", 3, 4), B("pc", 1, 2), 64.0, A.mult)
    ts(B("pc", 4, 5), B("pc", 0, 1), -16.0, A.mult)
    ts(B("pc", 5, 6), B("pc", 0, 1), 64.0, A.mult)
    for w in range(4):
        ts(B("pc", 9 + w, 10 + w), B("pc", 0, 1), 4.0, A.mult, float(w), A.add)
    tt(B("pc", 7, 8), B("pc", 3, 4), B("pc", 0, 1), A.subtract)
    ts(B("pc", 8, 9), B("pc", 7, 8), 15.0, A.add)
    ts(B("rev"), B("vs"), B("pc", 8, 9), A.is_equal)
    cp(B("kmf"), B("kmi"))
    for r in range(4):
        cp(B("kf", r, 64, 4), B("kmf", 3 - r, 64, 4))
    mm(B("pk", 0, 64), B("rev"), B("kf"))
    cp(B("k16_0"), B("pk", 0, 64))
    for q in range(16):
        ts(B("selc", 128 * q + q, 128 * q + 128, 16), B("g8"), grp, A.is_equal, 65536.0, A.mult)
    ts(B("idb"), B("idt"), 0.0, A.is_equal)
    ts(B("idf"), B("idt"), 0.0, A.is_equal)
    ts(B("sels"), B("selc"), 1.0 / 64, A.mult)
    ts(B("gbf"), B("gi"), grp, A.is_equal)
    cp(B("wtf", 0, 1), B("wti", 0, 1))
    ts(B("wb"), B("gbf"), B("wtf", 0, 1), A.mult)
    ts(B("mk"), B("r16"), q_, A.is_equal)
    ts(B("ra"), B("r16"), 0.5, A.is_gt)
    ts(B("rep4"), B("it8"), 0.0, A.mult, q4, A.add)
    ts(B("w68"), B("w68t"), B("pc", 4, 5), A.add)
    act(B("stab", 0, 1024), I(B("iot"), B("sl", 0, 64)))
    act(B("z", 0, 2560), I(B("trus"), B("sl", 0, 160)))
    cp(B("z", 2560, 4096), I(B("trus"), B("sl", 160, 256)))

    def consts():
        cp(B("val", 64, 68), B("w68", 64, 68))
        ts(B("nid"), B("idf"), -1.0, A.mult)
        cp(B("rep16"), B("it8"))
        ts(B("rw4"), B("it8"), 4.0, A.is_ge, 4.0, A.mult)
        ts(B("j16"), B("j16t"), B("pc", 5, 6), A.add)
        ts(B("rk2"), B("r16"), 0.0, A.is_equal, 2.0e9, A.mult)
        ts(B("repw"), B("rw4"), q4, A.add)
        ts(B("rk"), B("rk2"), -1.0e9, A.add)
        ts(B("dum"), B("dut"), q_, A.add)
        for r in range(4):
            for w in range(4):
                b = NB[r] + w * RW[r]
                ts(B("msk", b, b + 64), B("j16t"), B("pc", 9 + w, 10 + w), A.is_le)

    def ttg(a, b, t):
        cp(B("tt", 64 * a, 64 * b), I(B("bk"), B("k16_%d" % t, 4 * a, 4 * b)))

    def swap(p):
        lo, mid, hi = [int(64 * x) for x in PAIR[p]]
        for d, par in (("ta%d" % p, 0), ("tb%d" % p, 1)):
            for z, (a, b) in enumerate(((lo, mid), (mid, hi))):
                v = B("tt", a, b)
                dma("Y", T[d][z::2, :], T[v[0]][par::2, v[1]:v[2]], [v], [B(d)], z == 1)

    def gat(p, a, b, q):
        if p is None:
            o, i = B("gg", 1024 * a, 1024 * b), I(B("z"), B("tt", 64 * a, 64 * b))
            if q == "S":
                act(o, i)
            else:
                cp(o, i)
        else:
            o = 1024 * PAIR[p][0]
            act(B("gg", o + 1024 * a, int(o + 1024 * b)), I(B("z"), B("ta%d" % p, 64 * a, int(64 * b))))

    def fgat(p, a, b):
        a, b = int(1024 * a), int(1024 * b)
        o, m = 1024 * PAIR[p][0], int(1024 * PAIR[p][1])
        tt(B("gg", m + a, m + b), I(B("z"), B("tb%d" % p, a // 16, b // 16)), B("gg", o + a, o + b), A.min)

    def mins(a, b):
        scan(B("scn", 1024 * a, 1024 * b), B("rst", 0, 1024 * (b - a)), B("gg", 1024 * a, 1024 * b), 512.0, A.max, A.min)

    def pmins(p):
        lo, mid, hi = [int(1024 * x) for x in PAIR[p]]
        for z, a in ((0, lo), (1, mid)):
            scan(B("scn", a + 1, a + mid - lo, 2), B("rst", 0, mid - lo, 2), B("gg", mid + z, hi, 2), 512.0, A.max, A.min)

    def less(a, b):
        a = max(a, 1)
        tt(B("lt", 64 * a, 64 * b), B("scn", 1024 * a + 15, 1024 * b, 16), B("py", 0, 64 * (b - a)), A.is_lt)

    def st_gather(t):
        act(B("sg2"), I(B("stab"), B("src%d" % t)))

    def st_scatter(t):
        cp(I(B("stab"), B("dst%d" % t)), B("sg2"))

    thr = CB - 16390.0
    ttg(0, 1, 0)
    for t in range(VI):
        last = t == VI - 1
        K = "k16_%d" % t
        ttg(1, 2, t)
        ttg(6, 10, t)
        swap(0)
        gat(None, 0, 1, "S")
        gat(None, 1, 2, "S")
        ttg(2, 6, t)
        gat(None, 5, 6, "V")
        ttg(10, 14, t)
        ttg(14, 16, t)
        swap(1)
        gat(0, 0, 1, "S")
        if t:
            act(B("nwr"), I(B("nw", 0, 8), B("repw")))
        gat(0, 1, 2, "S")
        mins(0, 2)
        for k in range(4):
            mm(B("py", 64 * k, 64 * k + 64), B("idb"), B("scn", 15, 1024, 16))
        mm(B("pcn", 0, 64), B("cb"), B("on", 0, 64), True, False)
        if t:
            mm(B("pf", 0, 128), B("idf"), B("nwr"), True, False)
            mm(B("pf", 0, 128), B("nid"), B("ab%d" % (t - 1)), False, True)
        mins(5, 6)
        fgat(0, 0, 1)
        less(0, 2)
        less(5, 6)
        if t:
            for w in range(2):
                tt(B("ad2", 64 * w, 64 * w + 64), B("pf", 64 * w, 64 * w + 64), B("ohk"), A.mult)
            mm(B("pf", 0, 128), B("idf"), B("ab%d" % (t - 1)), True, False)
            mm(B("pf", 0, 128), B("idf"), B("ad2"), False, True)
        gat(1, 0, 1, "S")
        gat(1, 1, 2.5, "S")
        if t:
            act(B("abs%d" % (t - 1)), B("pf", 0, 128))
            send(nxt, "ab%d" % t, "abs%d" % (t - 1), "aa%d" % t)
            landed("ab%d" % t, prv, "aa%d" % t)
        fgat(0, 1, 2)
        pmins(0)
        if t == 0:
            consts()
        less(6, 10)
        fgat(1, 0, 1)
        gat(None, 15, 16, "S")
        gat(None, 2, 4, "S")
        gat(None, 4, 5, "S")
        fgat(1, 1, 2.5)
        cp(B("kf"), B(K))
        pmins(1)
        mm(B("pf", 0, 128), B("idf"), B("ab%d" % t))
        mins(15, 16)
        less(10, 13)
        less(13, 16)
        mins(2, 4)
        less(2, 4)
        mins(4, 5)
        less(4, 5)
        if t:
            st_gather(t - 1)
        act(B("scn", 16384 + 15, 17408, 16), B("scn", 1024 * (1 + t) + 15, 1024 * (2 + t), 16))
        if t == 0:
            for h in (1, 2):
                act(B("stab", 1024 * h, 1024 * h + 1024), I(B("iot"), B("sl", 64 * h, 64 * h + 64)))
        for q in range(16):
            mm(B("pcn", 0, 64), B("selc", 128 * q, 128 * q + 128), B("lt", q, 1024, 16), False, q == 15)
        mm(B("py", 0, 64), B("idf"), B("kf"), True, False)
        if t:
            st_scatter(t - 1)
        tt(B("val", 0, 64), B("pcn", 0, 64), B("w68", 0, 64), A.min)
        for r in range(4):
            red(B("m", r, r + 1), B("val", r, 68, 4), A.max)
        ts(B("off"), B("m", 0, 4), -1.0, A.mult, float(CB), A.add)
        ts(B("nh", 0, 4), B("m", 0, 4), thr, A.is_lt, 16384.0 - 1024.0 * (1 + t), A.mult)
        cp(B("ysel"), I(B("scn"), B("off")))
        mm(B("pu", 0, 64), B("wb"), B("ysel"))
        tt(B("m2", 0, 4), B("m", 0, 4), B("nh", 0, 4), A.add)
        ts(B("hit", 0, 4), B("m", 0, 4), thr, A.is_ge)
        tt(B("um"), B("pu", 0, 64), B("mk", 0, 64), A.mult)
        tt(B("ohk"), I(B("m2", 0, 4), B("rep4", 0, 4)), B("w68", 0, 64), A.is_equal)
        scan(B("us"), B("ra", 0, 64), B("um"), 0.0, A.mult, A.add)
        cp(B("ui", 0, 4), B("us", 15, 64, 16))
        ts(B("ua", 0, 4), B("ui", 0, 4), 4095, A.bitwise_and)
        for w in range(2):
            tt(B("pr", 64 * w, 64 * w + 64), B("pf", 64 * w, 64 * w + 64), B("ohk"), A.mult)
        for c in range(8):
            w, r = 1 - c // 4, c % 4
            act(B("prj", 16 * c, 16 * c + 16), B("pr", 64 * w + r, 64 * w + 64, 4), acc=B("old0", c, c + 1))
        ts(B("ux", 0, 4), B("ua", 0, 4), -2048.0, A.add)
        ts(B("uy", 0, 4), B("ua", 0, 4), 3232.0, A.add)
        tt(B("uz", 0, 4), B("ux", 0, 4), B("uy", 0, 4), A.mult)
        ts(B("un", 0, 4), B("uz", 0, 4), 5, A.arith_shift_right, 2047, A.bitwise_and)
        ts(B("nl", 0, 8, 2), B("un", 0, 4), B("cc", 0, 1), A.add)
        ts(B("nf", 0, 4), B("un", 0, 4), B("cc", 0, 1), A.add)
        act(B("nfr"), I(B("nf", 0, 4), B("rep4", 0, 4)))
        mm(B("pk", 0, 64), B("idf"), B("nfr"), True, False)
        mm(B("pk", 0, 64), B("nid"), B("kf"), False, True)
        for r in range(4):
            cp(B("e2", r, 64, 4), I(B("bk"), B("nl", 2 * r, 2 * r + 1)))
        for h in range(2):
            act(B("zg", 512 + 256 * h, 768 + 256 * h), I(B("z"), B("e2", 32 + 16 * h, 48 + 16 * h)))
            cp(B("zg", 256 * h, 256 * h + 256), I(B("z"), B("e2", 16 * h, 16 * h + 16)))
        order = [0, 1, 2, 3, 8, 9, 10, 11, 4, 5, 6, 7, 12, 13, 14, 15]
        for q in order:
            mm(B("psc", 0, 64), B("sels", 128 * q, 128 * q + 128), B("zg", 64 * q, 64 * q + 64), q == 0, q == 15)
        act(B("tr"), I(B("iot"), B("e2")))
        tt(B("old"), I(B("hit", 0, 4), B("rep4", 0, 1)), B("old0"), A.mult)
        tt(B("kd2"), B("pk", 0, 64), B("ohk"), A.mult)
        tt(B("rr"), I(B("old", 0, 8), B("rep16")), B("mk"), A.mult)
        mm(B("py", 0, 64), B("idf"), B("kd2"), False, True)
        mm(B("po", 0, 128), B("gbf"), B("rr"))
        mm(B("ph", 0, 4), B("on"), B("hit", 0, 4))
        tt(B("kab", 0, 64), B("j16"), B("psc", 0, 64), A.add)
        tt(B("kab", 64, 128), B("j16"), B("psc", 0, 64), A.subtract)
        for w in range(2):
            act(B("oth", 2 + w, 256, 4), B("po", 64 * w, 64 * w + 64), F.Identity, bias=8192.0)
        scan(B("kss"), B("rk"), B("kab"), 0.0, A.max, A.min)
        cp(B("ki"), B("kss", 15, 128, 16))
        ts(B("owo"), B("old", 0, 8), 8192.0, A.add, 4351.0, A.min)
        ts(B("ka"), B("ki"), 1023, A.bitwise_and)
        if not last:
            cp(B("ks%d" % (t + 1)), B("py", 0, 64))
            send(nxt, "k16_%d" % (t + 1), "ks%d" % (t + 1), "ak%d" % (t + 1))
            landed("k16_%d" % (t + 1), prv, "ak%d" % (t + 1))
        else:
            cp(B("kint"), B("py", 0, 64))
            ts(B("kin2"), B("kint"), 2047, A.bitwise_and)
        cp(B("ofn"), B("ka"))
        cp(B("src%d" % t, 8, 16), B("owo"))
        for w in range(2):
            act(B("oth", w, 256, 4), I(B("tr"), B("ofn", 4 * w, 4 * w + 4)))
        tt(B("om"), I(B("tr"), B("ofn")), B("mk"), A.mult)
        scan(B("osn"), B("ra"), B("om"), 0.0, A.mult, A.add)

        def own(w, r):
            return B("osn", 64 * w + 16 * r + 15, 64 * w + 16 * r + 16) if w < 2 else B("owo", 4 * w - 8 + r, 4 * w - 7 + r)

        def blk(w, r):
            return B("ne", NB[r] + w * RW[r], NB[r] + (w + 1) * RW[r])
        for r in range(4):
            for w in (2, 3) if r >= 2 else (2, 3, 1):
                act(blk(w, r), B("oth", 64 * r, 256), F.Square, bias=own(w, r), scale=-1.0)
        for r in range(4):
            for w in (0, 1) if r >= 2 else (0,):
                ts(blk(w, r), B("oth", 64 * r, 256), own(w, r), A.not_equal)
            if r == 0:
                cp(B("src%d" % t, 0, 8), B("osn", 15, 128, 16))
        if not last:
            act(B("zg2"), I(B("z"), B("src%d" % t)))
        for w in range(2):
            act(B("pd", 4 * w, 4 * w + 4), B("osn", 79 - 64 * w, 128 - 64 * w, 16), F.Identity, bias=-8192.0)
            act(B("pd", 8 + 4 * w, 12 + 4 * w), B("old", 4 - 4 * w, 8 - 4 * w))
        act(B("ccj", 0, 4), B("ph", 0, 4), acc=B("cc", 0, 1))
        for r in range(4):
            R = RW[r]
            scan(B("ns", NB[r], NB[r] + 4 * R), B("ne", NB[r], NB[r] + 4 * R), B("msk", NB[r], NB[r] + 4 * R), 1.0, A.min, A.max)
        for r in range(4):
            R = RW[r]
            red(B("acc", r, r + 1), B("ns", NB[r] + R - 1, NB[r] + 4 * R, R), A.min)
        if not last:
            ttg(0, 1, t + 1)
        tt(B("nw"), I(B("acc", 0, 4), B("rep4", 0, 1)), B("pd"), A.mult)
        tt(B("da"), B("nw"), B("dum"), A.min)
        if last:
            st_gather(t)
        ts(B("dst%d" % t), B("da"), 8192.0, A.add)
        if not last:
            cp(I(B("z"), B("dst%d" % t)), B("zg2"))
        if t == 0:
            act(B("stab", 3072, 4096), I(B("iot"), B("sl", 192, 256)))

    o = "ab%d" % (VI - 1)
    tt(B("ad"), I(B("nw", 0, 8), B("repw")), B(o), A.subtract)
    for w in range(2):
        tt(B("ad2", 64 * w, 64 * w + 64), B("ad", 64 * w, 64 * w + 64), B("ohk"), A.mult)
    tt(B("fa"), B(o), B("ad2"), A.add)
    ts(B("fn"), B("fa"), 0.0, A.is_equal, -8193.0, A.mult)
    mm(B("pf", 0, 128), B("rev"), B("fa"), True, False)
    mm(B("pf", 0, 128), B("rev"), B("fn"), False, True)
    for r in range(4):
        cp(B("kd", r, 64, 4), B("kin2", 3 - r, 64, 4))
    mm(B("pk", 0, 64), B("rev"), B("kd"))
    for r in range(4):
        ts(B("sna", r, 128, 4), B("pf", 3 - r, 128, 4), 8192.0, A.add)
    send(prv, "lna", "sna", "aa%d" % VI)
    cp(B("snk"), B("pk", 0, 64))
    send(prv, "lnk", "snk", "ak%d" % VI)
    st_scatter(VI - 1)
    landed("lnk", nxt, "ak%d" % VI)
    landed("lna", nxt, "aa%d" % VI)
    ends = [dma("Y", T.ys[:], T.stab[::16, 0:4096], [B("stab")], []),
            dma("S", T.ya[:], ap(B("lna", 0, 64)), [B("lna")], []),
            dma("S", T.yb[:], ap(B("lna", 64, 128)), [B("lna")], []),
            dma("Y", T.yk[:], T.lnk[:], [B("lnk")], [])]
    for q, s in ends:
        eng[q].wait_ge(T.sem[s], 16)
    g.wait_ge(T.sem["loc"], locs[0])
    for q in cnt:
        if known["Y"].get("q" + q, 0) < cnt[q]:
            g.sync.wait_ge(T.sem["q" + q], cnt[q])
